import numpy as np
import ml_dtypes


def mxq(x, axis, fmt="e4m3"):
    dtype, down = {"e4m3": (ml_dtypes.float8_e4m3fn, 7), "e5m2": (ml_dtypes.float8_e5m2, 14)}[fmt]
    v = np.moveaxis(np.asarray(x, np.float32).astype(ml_dtypes.bfloat16).astype(np.float64), axis, -1)
    blocks = v.reshape(v.shape[:-1] + (-1, 32))
    amax = np.abs(blocks).max(-1, keepdims=True)
    byte = np.maximum(np.where(amax > 0, np.frexp(amax)[1] - 1 + 127, 0) - down, 1)
    scale = np.exp2(byte - 127.0)
    codes = (blocks / scale).astype(np.float32).astype(dtype).astype(np.float64)
    return np.moveaxis((codes * scale).reshape(v.shape), -1, axis)


WIDE = False


def mx_kscale(k):
    if not WIDE:
        return np.ones(k)
    levels = np.array([10, -10, 5, -5, 0])
    if k % 512:
        return np.exp2(np.random.permutation(np.resize(levels, k // 32))).repeat(32)
    a = np.empty((k // 512, 16))
    for p in range(k // 512):
        a[p, :8] = np.random.permutation(np.resize(levels, 8))
        for g in range(8):
            far = levels[np.abs(levels - a[p, g]) >= 10]
            a[p, g + 8] = far[np.random.randint(len(far))]
    return np.exp2(a.ravel()).repeat(32)


def f64(x):
    return np.asarray(x).astype(np.float64)


def striped(idx):
    return np.tile(idx.reshape(-1, 16).T, (8, 1)).astype(np.uint16)


def unstriped(offs):
    return offs[:16].T.reshape(-1).astype(np.int64)


E2M1 = np.array([0.0, 0.5, 1.0, 1.5, 2.0, 3.0, 4.0, 6.0, -0.0, -0.5, -1.0, -1.5, -2.0, -3.0, -4.0, -6.0])


def pack_weight(w, fmt):
    k, n = w.shape
    w = f64(np.asarray(w, np.float32).astype(ml_dtypes.bfloat16)).reshape(k // 32, 32, n)
    amax = np.abs(w).max(1)
    if fmt == "e4m3":
        byte = np.frexp(amax)[1] - 1 + 127 - 7
    else:
        mant, ex = np.frexp(amax / 6.0)
        byte = np.where(mant > 0.5, ex, ex - 1) + 127
    byte = np.clip(np.where(amax > 0, byte, 1), 1, 254)
    scaled = (w * np.exp2(127.0 - byte)[:, None, :]).reshape(k, n).astype(np.float32)
    by_word = np.ascontiguousarray(scaled.reshape(k // 512, 128, 4, n).transpose(0, 1, 3, 2))
    if fmt == "e4m3":
        words = by_word.astype(ml_dtypes.float8_e4m3fn).view(np.uint8)
    else:
        c = by_word.astype(ml_dtypes.float4_e2m1fn).view(np.uint8) & 0xF
        words = (c[..., 0::2] | (c[..., 1::2] << 4)).reshape(k // 512, 128, 2 * n)
    return np.ascontiguousarray(words), np.ascontiguousarray(byte.astype(np.uint8).reshape(k // 512, 16, n))


def unpack_weight(words, scales, fmt):
    g, _, n = scales.shape
    words = np.ascontiguousarray(words).reshape(g, 128, n, -1)
    if fmt == "e4m3":
        vals = words.view(ml_dtypes.float8_e4m3fn).astype(np.float64)
    else:
        nib = np.empty((g, 128, n, 4), np.uint8)
        nib[..., 0::2] = words & 0xF
        nib[..., 1::2] = words >> 4
        vals = E2M1[nib]
    vals = vals * np.repeat(np.exp2(scales.astype(np.float64) - 127.0), 8, axis=1)[..., None]
    return vals.transpose(0, 1, 3, 2).reshape(g * 512, n)


def gelu(v):
    return 0.5 * v * (1.0 + np.tanh(np.sqrt(2.0 / np.pi) * (v + 0.044715 * v**3)))


K, KB, T, TB, S, H, T2, N, P = 1024, 512, 2048, 1024, 512, 1024, 2048, 512, 1024

def setup_inputs():
    n = np.random.standard_normal
    s, sb, u = mx_kscale(K)[:, None], mx_kscale(KB)[:, None], mx_kscale(H)[:, None]
    d = {}
    d["tab_words"], d["tab_scales"] = pack_weight(n((K, T)) * s, "e4m3")
    d["tab2_words"], d["tab2_scales"] = pack_weight(n((KB, TB)) * sb, "e4m3")
    d["offs"] = striped(np.random.permutation(T)[:S])
    d["offs2"] = striped(np.random.permutation(TB)[:S])
    perm = np.random.permutation(T2)
    d["offs3"] = striped(perm[:S])
    d["offs4"] = striped(perm[S:2 * S])
    d["offs5"] = striped(np.random.permutation(T2)[:P])
    d["w1"] = (3.0 * n((K, H)) / K**0.5 / s).astype(np.float32)
    d["wf"] = (3.0 * np.exp(0.3 * n(H)) * u[:, 0]).astype(np.float32)
    d["w2_words"], d["w2_scales"] = pack_weight(2.0 * n((KB, H)) / KB**0.5 / sb, "e2m1")
    d["wp"] = (np.exp(0.3 * n(H)) * u[:, 0]).astype(np.float32)
    d["wg1"] = np.exp(0.3 * n((128, S))).astype(np.float32)
    d["wg2"] = np.exp(0.3 * n((128, S))).astype(np.float32)
    d["page0"] = (0.8 * n((H, T2)) * u).astype(np.float32)
    d["base"] = (0.7 * n((H, P)) * u).astype(np.float32)
    d["w3"] = (n((H, N)) / H**0.5 / u).astype(np.float32)
    return d

def reference(tab_words, tab_scales, tab2_words, tab2_scales, offs, offs2, offs3, offs4, offs5,
              w1, wf, w2_words, w2_scales, wp, wg1, wg2, page0, base, w3):
    v = unpack_weight(tab_words, tab_scales, "e4m3")[:, unstriped(offs)]
    v2 = unpack_weight(tab2_words, tab2_scales, "e4m3")[:, unstriped(offs2)]
    feed = mxq(f64(w1), 0, "e4m3").T @ v
    h1 = f64(wf)[:, None] / (1.0 + np.exp(-feed))
    pres = unpack_weight(w2_words, w2_scales, "e2m1").T @ v2
    h2 = f64(wp)[:, None] * np.sqrt(1.0 + np.square(pres))
    page = f64(page0).copy()
    page[:, unstriped(offs3)] = np.tile(f64(wg1), (H // 128, 1)) * h1
    page[:, unstriped(offs4)] = np.tile(f64(wg2), (H // 128, 1)) * h2
    x = page[:, unstriped(offs5)] - f64(base)
    return mxq(f64(w3), 0, "e4m3").T @ mxq(x, 0, "e4m3")

@@ -1,0 +1,337 @@
+from contextlib import ExitStack
+
+import concourse.mybir as mybir
+from concourse.masks import make_identity
+
+K, KB, T, TB, S, H, T2, N, M = 1024, 512, 2048, 1024, 512, 1024, 2048, 512, 1024
+FLOPS = 2 * (K * H * S + KB * H * S + H * N * M)
+
+F32 = mybir.dt.float32
+BF16 = mybir.dt.bfloat16
+I32 = mybir.dt.int32
+U32 = mybir.dt.uint32
+U16 = mybir.dt.uint16
+U8 = mybir.dt.uint8
+FP8X4 = mybir.dt.float8_e4m3fn_x4
+FP4X4 = mybir.dt.float4_e2m1fn_x4
+ACT = mybir.ActivationFunctionType
+ALU = mybir.AluOpType
+
+P = 128
+PACK = 4
+PASS = P * PACK
+ROW_TILES = H // P
+LAST = ROW_TILES - 1
+CHUNKS = ((0, 512), (512, 256), (768, 128), (896, 128))
+
+
+def tile_list_membrane_fouling_slots_kernel(
+    tc, tab_words, tab_scales, tab2_words, tab2_scales, offs, offs2, offs3, offs4, offs5,
+    w1, wf, w2_words, w2_scales, wp, wg1, wg2, page0, base, w3, out,
+):
+    nc = tc.nc
+    with ExitStack() as ctx:
+        keep = ctx.enter_context(tc.tile_pool(name="keep", bufs=1))
+        ring = ctx.enter_context(tc.tile_pool(name="ring", bufs=2))
+        psum = ctx.enter_context(tc.psum_pool(name="psum", bufs=1))
+
+        def load_list(src, name):
+            lst = keep.tile(list(src.shape), U16, name=name)
+            nc.sync.dma_start(lst[:], src)
+            return lst
+
+        def load_words(src, width, name):
+            words = keep.tile([P, width], U32, name=name, align_bytes=64)
+            nc.sync.dma_start(words[:].bitcast(I32), src.rearrange("p t i -> p (t i)").bitcast(I32))
+            return words
+
+        def load_scale_rows(src, width, name):
+            plane = keep.tile([P, width], U8, name=name, align_bytes=64)
+            for q in range(4):
+                nc.sync.dma_start(
+                    plane[32 * q : 32 * q + 32, :].bitcast(I32),
+                    src[4 * q : 4 * q + 4, :].bitcast(I32).partition_broadcast(8),
+                )
+            return plane
+
+        def load_channel_weights(src, name):
+            vec = keep.tile([P, H // PASS, PACK], F32, name=name)
+            nc.sync.dma_start(vec[:], src.rearrange("(b p t) -> p b t", p=P, t=PACK))
+            return vec
+
+        def load_page(i):
+            b, t = divmod(i, PACK)
+            page = keep.tile([P, T2], F32, name="page%d" % i)
+            rows = page0[b * PASS : (b + 1) * PASS, :].rearrange("(p t) s -> p t s", t=PACK)
+            nc.sync.dma_start(page[:], rows[:, t, :])
+            return page
+
+        def load_rows(src, g, cols, tag):
+            width = cols.stop - cols.start
+            raw = keep.tile([P, PACK, width], F32, name="rows", tag=tag)
+            rows = src[g * PASS : (g + 1) * PASS, :].rearrange("(p t) c -> p t c", t=PACK)
+            nc.sync.dma_start(raw[:], rows[:, :, cols])
+            return raw
+
+        def load_gain(src, name):
+            gain = keep.tile([P, S], F32, name=name)
+            nc.sync.dma_start(gain[:], src)
+            return gain
+
+        def gather(window, lst, dtype, name):
+            picked = keep.tile([P, S], dtype, name=name, align_bytes=64)
+            nc.vector.tensor_copy(picked[:], window[:].indirect(lst[:]))
+            return picked
+
+        def quantize(grouped, pool, name):
+            width = grouped.shape[1] // PACK
+            codes = pool.tile([P, width], U32, name=name + "_codes", align_bytes=64)
+            scales = pool.tile([P, width], U8, name=name + "_scales", align_bytes=64)
+            nc.vector.quantize_mx(out=codes[:].bitcast(FP8X4), scales=scales[:], in_=grouped[:])
+            return codes, scales
+
+        def interleave(raw):
+            width = raw.shape[2]
+            grouped = ring.tile([P, PACK * width], BF16, name="grouped", align_bytes=64)
+            nc.scalar.copy(
+                grouped[:].rearrange("p (c i t) -> p c t i", i=4, t=PACK),
+                raw[:].rearrange("p t (c i) -> p c t i", i=4),
+            )
+            return grouped
+
+        def interleave_dealt(raw):
+            grouped = ring.tile([P, PACK * PASS], BF16, name="grouped", align_bytes=64)
+            nc.scalar.copy(
+                grouped[:].rearrange("p (t m j) -> p m j t", t=PACK, j=PACK),
+                raw[:].rearrange("p j (m t) -> p m j t", t=PACK),
+            )
+            return grouped
+
+        def turn_gain(gain):
+            bank = psum.tile([P, S // P, P], F32, name="turned")
+            for c in range(S // P):
+                nc.tensor.transpose(bank[:, c, :], gain[:, c * P : (c + 1) * P], ident[:])
+            return bank
+
+        def repeat_gain(bank, t):
+            rep = keep.tile([P, S // P, 4, 32], F32, name="repeated", tag="repeated%d" % t)
+            rows = bank[:].rearrange("p c (a t) -> p c t a", t=PACK)[:, :, t : t + 1, :]
+            nc.scalar.copy(rep[:], rows.to_broadcast([P, S // P, 4, 32]))
+            return rep
+
+        def operands(i):
+            if i == LAST:
+                return ring.tile([P, 2, S], F32, name="operands", tag="picked")
+            return keep.tile([P, 2, S], F32, name="operands", tag="operands%d" % i)
+
+        def scaled_gain(rep, weights, i, dst):
+            b, t = divmod(i, PACK)
+            bank = psum.tile([P, S], F32, name="bank", bufs=7)
+            for c in range(S // P):
+                nc.tensor.transpose(
+                    bank[:, c * P : (c + 1) * P], rep[:, c, :, :].rearrange("p q a -> p (q a)"), ident[:]
+                )
+            nc.scalar.activation(dst, bank[:], ACT.Copy, scale=weights[:, b, t : t + 1])
+
+        ident = keep.tile([P, P], F32, name="ident")
+        make_identity(nc, ident[:])
+        zero = keep.tile([P, 1], F32, name="zero")
+        zero_root = keep.tile([P, 1], F32, name="zero_root")
+        nc.vector.memset(zero[:], 0.0)
+        nc.scalar.activation(zero_root[:], zero[:], ACT.Sqrt)
+        tab_plane = keep.tile([P, T], U8, name="tab_plane", align_bytes=64)
+        nc.vector.memset(tab_plane[:].bitcast(I32), 0)
+
+        w2_raw = keep.tile([P, 2 * H], U8, name="w2_raw")
+        nc.sync.dma_start(w2_raw[:].bitcast(I32), w2_words[0].bitcast(I32))
+        tab2_sb = load_words(tab2_words[0], TB, "tab2_sb")
+        wg2_sb = load_gain(wg2, "wg2_sb")
+        idx2 = load_list(offs2, "idx2")
+        tab2_plane = load_scale_rows(tab2_scales[0], TB, "tab2_plane")
+        pages = [load_page(0)]
+        w2_plane = load_scale_rows(w2_scales[0], H, "w2_plane")
+        wp_sb = load_channel_weights(wp, "wp_sb")
+        idx4 = load_list(offs4, "idx4")
+        pages.append(load_page(1))
+        idx = load_list(offs, "idx")
+        tab_sb = [load_words(tab_words[0], T, "tab_sb0")]
+        pages.append(load_page(2))
+        for q in range(4):
+            nc.sync.dma_start(
+                tab_plane[32 * q : 32 * q + 8, :].bitcast(I32),
+                tab_scales[:, 4 * q : 4 * q + 4, :].bitcast(I32),
+            )
+        tab_sb.append(load_words(tab_words[1], T, "tab_sb1"))
+        pages.append(load_page(3))
+        w1_raw = {}
+        for a in range(2):
+            w1_raw[a, 0] = load_rows(w1, a, slice(0, PASS), "stage%d" % a)
+        pages.append(load_page(4))
+        wg1_sb = load_gain(wg1, "wg1_sb")
+        wf_sb = load_channel_weights(wf, "wf_sb")
+        idx3 = load_list(offs3, "idx3")
+        pages.append(load_page(5))
+        pages.append(load_page(6))
+        for a in range(2):
+            w1_raw[a, 1] = load_rows(w1, a, slice(PASS, H), "stage%d" % (2 + a))
+        idx5 = load_list(offs5, "idx5")
+        base_sb = {}
+        for c in range(1, len(CHUNKS)):
+            m0, width = CHUNKS[c]
+            for b in range(2):
+                base_sb[c, b] = load_rows(base, b, slice(m0, m0 + width), "base%d_%d" % (c, b))
+
+        w2_codes = keep.tile([P, 2 * H], U8, name="w2_codes", align_bytes=64)
+        w2_sc = keep.tile([P, H], U8, name="w2_sc", align_bytes=64)
+
+        def deal_w2_codes(b):
+            cols = slice(2 * b * PASS, 2 * (b + 1) * PASS)
+            nc.vector.tensor_copy(
+                w2_codes[:, cols].rearrange("p (t m e) -> p t m e", t=PACK, e=2),
+                w2_raw[:, cols].rearrange("p (m t e) -> p t m e", t=PACK, e=2),
+            )
+
+        def deal_w2_scales(b):
+            cols = slice(b * PASS, (b + 1) * PASS)
+            nc.vector.tensor_copy(
+                w2_sc[:, cols].rearrange("p (t m) -> p t m", t=PACK),
+                w2_plane[:, cols].rearrange("p (m t) -> p t m", t=PACK),
+            )
+
+        deal_w2_codes(0)
+        v2_codes = gather(tab2_sb, idx2, U32, "v2_codes")
+        v2_sc = gather(tab2_plane, idx2, U8, "v2_sc")
+        deal_w2_scales(0)
+        deal_w2_codes(1)
+        deal_w2_scales(1)
+        wg2_turned = turn_gain(wg2_sb)
+        wg2_rep = {}
+        pres_ops = {}
+
+        def pressure_operands(i):
+            t = i % PACK
+            ops = operands(i)
+            bank = psum.tile([P, S], F32, name="bank", bufs=7)
+            nc.tensor.matmul_mx(
+                out=bank[:],
+                lhsT=w2_codes[:, 2 * i * P : 2 * (i + 1) * P].bitcast(FP4X4),
+                lhsT_scale=w2_sc[:, i * P : (i + 1) * P],
+                rhs=v2_codes[:].bitcast(FP8X4),
+                rhs_scale=v2_sc[:],
+                start=True,
+                stop=True,
+            )
+            if t not in wg2_rep:
+                wg2_rep[t] = repeat_gain(wg2_turned, t)
+            scaled_gain(wg2_rep[t], wp_sb, i, ops[:, 0, :])
+            nc.scalar.activation(ops[:, 1, :], bank[:], ACT.Square, bias=zero_root[:])
+            nc.scalar.activation(ops[:, 1, :], ops[:, 1, :], ACT.Sqrt, bias=1.0)
+            pres_ops[i] = ops
+
+        def scatter(i, lst, ops):
+            nc.vector.tensor_tensor(pages[i][:].indirect(lst[:]), ops[:, 1, :], ops[:, 0, :], ALU.mult)
+
+        w1_q = {}
+
+        def quantize_w1(a, b):
+            w1_q[a, b] = quantize(interleave_dealt(w1_raw[a, b]), keep, "w1_%d%d" % (a, b))
+
+        for i in range(2):
+            pressure_operands(i)
+            scatter(i, idx4, pres_ops[i])
+        v_codes = [gather(tab_sb[0], idx, U32, "v_codes0")]
+        pressure_operands(2)
+        scatter(2, idx4, pres_ops[2])
+        v_sc = gather(tab_plane, idx, U8, "v_sc")
+        v_codes.append(gather(tab_sb[1], idx, U32, "v_codes1"))
+        for i in range(3, 6):
+            pressure_operands(i)
+            scatter(i, idx4, pres_ops[i])
+        for a in range(2):
+            quantize_w1(a, 0)
+        pressure_operands(6)
+        scatter(6, idx4, pres_ops[6])
+        pressure_operands(LAST)
+
+        wg1_turned = turn_gain(wg1_sb)
+        wg1_rep = {}
+
+        def feed_operands(i):
+            b, t = divmod(i, PACK)
+            ops = operands(i)
+            bank = psum.tile([P, S], F32, name="bank", bufs=7)
+            for a in range(2):
+                codes, scales = w1_q[a, b]
+                nc.tensor.matmul_mx(
+                    out=bank[:],
+                    lhsT=codes[:, t * P : (t + 1) * P].bitcast(FP8X4),
+                    lhsT_scale=scales[:, t * P : (t + 1) * P],
+                    rhs=v_codes[a][:].bitcast(FP8X4),
+                    rhs_scale=v_sc[4 * a : P, :],
+                    start=(a == 0),
+                    stop=(a == 1),
+                )
+            if t not in wg1_rep:
+                wg1_rep[t] = repeat_gain(wg1_turned, t)
+            scaled_gain(wg1_rep[t], wf_sb, i, ops[:, 0, :])
+            nc.scalar.activation(ops[:, 1, :], bank[:], ACT.Sigmoid)
+            return ops
+
+        for i in range(PACK):
+            scatter(i, idx3, feed_operands(i))
+        for b in range(2):
+            base_sb[0, b] = load_rows(base, b, slice(0, CHUNKS[0][1]), "stage%d" % b)
+        for a in range(2):
+            quantize_w1(a, 1)
+        w3_raw = [load_rows(w3, b, slice(0, N), "stage%d" % (2 + b)) for b in range(2)]
+        pages.append(load_page(LAST))
+        for i in range(PACK, LAST):
+            scatter(i, idx3, feed_operands(i))
+        last_feed = feed_operands(LAST)
+        w3_q = [quantize(interleave(w3_raw[b]), keep, "w3_%d" % b) for b in range(2)]
+        scatter(LAST, idx4, pres_ops[LAST])
+        scatter(LAST, idx3, last_feed)
+
+        def pick(c, b):
+            m0, width = CHUNKS[c]
+            picked = ring.tile([P, PACK, width], F32, name="picked", tag="picked")
+            lst = idx5[:, m0 // 16 : (m0 + width) // 16]
+            for t in range(PACK):
+                nc.vector.tensor_tensor(
+                    picked[:, t, :], pages[PACK * b + t][:].indirect(lst), base_sb[c, b][:, t, :], ALU.subtract
+                )
+            return interleave(picked)
+
+        out_rows = out.rearrange("(n p) m -> p n m", p=P)
+        banks = {}
+
+        def multiply(c, b, grouped):
+            m0, width = CHUNKS[c]
+            x_codes, x_scales = quantize(grouped, ring, "x")
+            codes, scales = w3_q[b]
+            for n in range(N // P):
+                if b == 0:
+                    banks[n] = psum.tile([P, width], F32, name="bank", bufs=7)
+                nc.tensor.matmul_mx(
+                    out=banks[n][:],
+                    lhsT=codes[:, n * P : (n + 1) * P].bitcast(FP8X4),
+                    lhsT_scale=scales[:, n * P : (n + 1) * P],
+                    rhs=x_codes[:].bitcast(FP8X4),
+                    rhs_scale=x_scales[:],
+                    start=(b == 0),
+                    stop=(b == 1),
+                )
+            if b == 1:
+                tag = "stage0" if c == 0 else "base%d_0" % c
+                result = keep.tile([P, N // P, width], F32, name="result", tag=tag)
+                for n in range(N // P):
+                    nc.scalar.copy(result[:, n, :], banks[n][:])
+                nc.sync.dma_start(out_rows[:, :, m0 : m0 + width], result[:])
+
+        units = [(c, b) for c in range(len(CHUNKS)) for b in range(2)]
+        waiting = pick(*units[0])
+        for u in range(1, len(units)):
+            picked_next = pick(*units[u])
+            multiply(*units[u - 1], waiting)
+            waiting = picked_next
+        multiply(*units[-1], waiting)

@@ -32,21 +32,24 @@ def tile_list_membrane_fouling_slots_kernel(
     nc = tc.nc
     with ExitStack() as ctx:
         keep = ctx.enter_context(tc.tile_pool(name="keep", bufs=1))
-        ring = ctx.enter_context(tc.tile_pool(name="ring", bufs=2))
         psum = ctx.enter_context(tc.psum_pool(name="psum", bufs=1))
+
+        def held(shape, dtype, tag):
+            return keep.tile(shape, dtype, name=tag, tag=tag, align_bytes=64)
+
+        def new_bank(width=S):
+            return psum.tile([P, width], F32, name="bank", bufs=8)
 
         def load_list(src, name):
             lst = keep.tile(list(src.shape), U16, name=name)
             nc.sync.dma_start(lst[:], src)
             return lst
 
-        def load_words(src, width, name):
-            words = keep.tile([P, width], U32, name=name, align_bytes=64)
-            nc.sync.dma_start(words[:].bitcast(I32), src.rearrange("p t i -> p (t i)").bitcast(I32))
-            return words
+        def load_words(dst, src):
+            nc.sync.dma_start(dst.bitcast(I32), src.rearrange("p t i -> p (t i)").bitcast(I32))
 
         def load_scale_rows(src, width, name):
-            plane = keep.tile([P, width], U8, name=name, align_bytes=64)
+            plane = held([P, width], U8, name)
             for q in range(4):
                 nc.sync.dma_start(
                     plane[32 * q : 32 * q + 32, :].bitcast(I32),
@@ -54,164 +57,174 @@ def tile_list_membrane_fouling_slots_kernel(
                 )
             return plane
 
-        def load_channel_weights(src, name):
-            vec = keep.tile([P, H // PASS, PACK], F32, name=name)
-            nc.sync.dma_start(vec[:], src.rearrange("(b p t) -> p b t", p=P, t=PACK))
-            return vec
+        def load_channel_weights(src, name, queue):
+            rows = keep.tile([P, P], F32, name=name)
+            nc.gpsimd.memset(rows[:], 0.0)
+            for b in range(2):
+                queue.dma_start(
+                    rows[PACK * b : PACK * (b + 1), :].rearrange("t (q j) -> t q j", j=8),
+                    src[b * PASS : (b + 1) * PASS].rearrange("(q t j) -> t q j", t=PACK, j=8),
+                )
+            return rows
+
+        def turn_channel_weights(rows, name):
+            bank = new_bank(P)
+            nc.tensor.transpose(bank[:], rows[:], ident[:])
+            columns = keep.tile([P, ROW_TILES], F32, name=name)
+            nc.scalar.copy(columns[:], bank[:, :ROW_TILES])
+            return columns
+
+        def pass_rows(src, g):
+            return src[g * PASS : (g + 1) * PASS, :].rearrange("(p t) c -> p t c", t=PACK)
+
+        def slot_rows(src, b, t):
+            return src[b * PASS : (b + 1) * PASS, :].rearrange("(q t j) c -> t q j c", t=PACK, j=8)[t]
 
         def load_page(i):
             b, t = divmod(i, PACK)
-            page = keep.tile([P, T2], F32, name="page%d" % i)
-            rows = page0[b * PASS : (b + 1) * PASS, :].rearrange("(p t) s -> p t s", t=PACK)
-            nc.sync.dma_start(page[:], rows[:, t, :])
+            page = held([P, T2], F32, "page%d" % i)
+            nc.sync.dma_start(page[:], slot_rows(page0, b, t))
             return page
 
-        def load_rows(src, g, cols, tag):
-            width = cols.stop - cols.start
-            raw = keep.tile([P, PACK, width], F32, name="rows", tag=tag)
-            rows = src[g * PASS : (g + 1) * PASS, :].rearrange("(p t) c -> p t c", t=PACK)
-            nc.sync.dma_start(raw[:], rows[:, :, cols])
+        def load_w1(a, b):
+            raw = held([P, PACK, PASS], F32, "late_room" if (a, b) == (1, 0) else "stage%d" % (2 * b + a))
+            nc.sync.dma_start(raw[:], pass_rows(w1, a)[:, :, b * PASS : (b + 1) * PASS])
             return raw
+
+        def load_base(b, u):
+            rows = held([P, 2, M], F32, "stage%d" % (2 * b + u))
+            for e in range(2):
+                nc.sync.dma_start(rows[:, e, :], slot_rows(base, b, 2 * u + e))
+            return rows
 
         def load_gain(src, name):
             gain = keep.tile([P, S], F32, name=name)
             nc.sync.dma_start(gain[:], src)
             return gain
 
-        def gather(window, lst, dtype, name):
-            picked = keep.tile([P, S], dtype, name=name, align_bytes=64)
-            nc.vector.tensor_copy(picked[:], window[:].indirect(lst[:]))
+        def gather(window, lst, dtype, tag):
+            picked = held([P, S], dtype, tag)
+            nc.vector.tensor_copy(picked[:], window.indirect(lst[:]))
             return picked
 
-        def quantize(grouped, pool, name):
+        def quantize(grouped, codes_tag, scales_tag):
             width = grouped.shape[1] // PACK
-            codes = pool.tile([P, width], U32, name=name + "_codes", align_bytes=64)
-            scales = pool.tile([P, width], U8, name=name + "_scales", align_bytes=64)
-            nc.vector.quantize_mx(out=codes[:].bitcast(FP8X4), scales=scales[:], in_=grouped[:])
+            codes = held([P, width], U32, codes_tag)
+            scales = held([P, width], U8, scales_tag)
+            nc.vector.quantize_mx(out=codes[:].bitcast(FP8X4), scales=scales[:], in_=grouped)
             return codes, scales
 
-        def interleave(raw):
-            width = raw.shape[2]
-            grouped = ring.tile([P, PACK * width], BF16, name="grouped", align_bytes=64)
-            nc.scalar.copy(
-                grouped[:].rearrange("p (c i t) -> p c t i", i=4, t=PACK),
-                raw[:].rearrange("p t (c i) -> p c t i", i=4),
+        def interleave(copy, grouped, raw):
+            copy(
+                grouped.rearrange("p (c i t) -> p c t i", i=4, t=PACK),
+                raw.rearrange("p t (c i) -> p c t i", i=4),
             )
-            return grouped
 
-        def interleave_dealt(raw):
-            grouped = ring.tile([P, PACK * PASS], BF16, name="grouped", align_bytes=64)
+        def interleave_dealt(grouped, raw):
             nc.scalar.copy(
-                grouped[:].rearrange("p (t m j) -> p m j t", t=PACK, j=PACK),
-                raw[:].rearrange("p j (m t) -> p m j t", t=PACK),
+                grouped.rearrange("p (t q j a) -> p q t a j", t=PACK, j=8, a=PACK),
+                raw.rearrange("p a (q t j) -> p q t a j", t=PACK, j=8),
             )
-            return grouped
 
         def turn_gain(gain):
-            bank = psum.tile([P, S // P, P], F32, name="turned")
+            bank = new_bank()
             for c in range(S // P):
-                nc.tensor.transpose(bank[:, c, :], gain[:, c * P : (c + 1) * P], ident[:])
+                nc.tensor.transpose(bank[:, c * P : (c + 1) * P], gain[:, c * P : (c + 1) * P], ident[:])
             return bank
 
-        def repeat_gain(bank, t):
-            rep = keep.tile([P, S // P, 4, 32], F32, name="repeated", tag="repeated%d" % t)
-            rows = bank[:].rearrange("p c (a t) -> p c t a", t=PACK)[:, :, t : t + 1, :]
-            nc.scalar.copy(rep[:], rows.to_broadcast([P, S // P, 4, 32]))
+        def repeat_gain(bank, t, rep):
+            rows = bank[:].rearrange("p (c q t j) -> p c t q j", c=S // P, t=PACK, j=8)[:, :, t : t + 1]
+            rep = rep.rearrange("p (c r q j) -> p c r q j", c=S // P, r=4, q=4)
+            nc.scalar.copy(rep, rows.to_broadcast([P, S // P, 4, 4, 8]))
             return rep
 
-        def operands(i):
-            if i == LAST:
-                return ring.tile([P, 2, S], F32, name="operands", tag="picked")
-            return keep.tile([P, 2, S], F32, name="operands", tag="operands%d" % i)
-
-        def scaled_gain(rep, weights, i, dst):
-            b, t = divmod(i, PACK)
-            bank = psum.tile([P, S], F32, name="bank", bufs=7)
+        def scaled_gain(rep, weights, i, gain):
+            bank = new_bank()
             for c in range(S // P):
                 nc.tensor.transpose(
-                    bank[:, c * P : (c + 1) * P], rep[:, c, :, :].rearrange("p q a -> p (q a)"), ident[:]
+                    bank[:, c * P : (c + 1) * P], rep[:, c].rearrange("p r q j -> p (r q j)"), ident[:]
                 )
-            nc.scalar.activation(dst, bank[:], ACT.Copy, scale=weights[:, b, t : t + 1])
+            nc.scalar.activation(gain, bank[:], ACT.Copy, scale=weights[:, i : i + 1])
 
+        def scatter(i, lst, gain, h):
+            nc.vector.tensor_tensor(pages[i][:].indirect(lst[:]), h, gain, ALU.mult)
+
+
+        wp_rows = load_channel_weights(wp, "wp_rows", nc.gpsimd)
         ident = keep.tile([P, P], F32, name="ident")
         make_identity(nc, ident[:])
         zero = keep.tile([P, 1], F32, name="zero")
         zero_root = keep.tile([P, 1], F32, name="zero_root")
         nc.vector.memset(zero[:], 0.0)
         nc.scalar.activation(zero_root[:], zero[:], ACT.Sqrt)
-        tab_plane = keep.tile([P, T], U8, name="tab_plane", align_bytes=64)
+        tab_plane = held([P, T], U8, "tab_plane")
         nc.vector.memset(tab_plane[:].bitcast(I32), 0)
 
-        w2_raw = keep.tile([P, 2 * H], U8, name="w2_raw")
-        nc.sync.dma_start(w2_raw[:].bitcast(I32), w2_words[0].bitcast(I32))
-        tab2_sb = load_words(tab2_words[0], TB, "tab2_sb")
-        wg2_sb = load_gain(wg2, "wg2_sb")
+        tab2_sb = held([P, TB], U32, "tab2_sb")
+        load_words(tab2_sb[:], tab2_words[0])
         idx2 = load_list(offs2, "idx2")
         tab2_plane = load_scale_rows(tab2_scales[0], TB, "tab2_plane")
-        pages = [load_page(0)]
+        w2_raw = keep.tile([P, 2 * H], U8, name="w2_raw")
+        nc.sync.dma_start(w2_raw[:].bitcast(I32), w2_words[0].bitcast(I32))
+        wg2_sb = load_gain(wg2, "wg2_sb")
         w2_plane = load_scale_rows(w2_scales[0], H, "w2_plane")
-        wp_sb = load_channel_weights(wp, "wp_sb")
         idx4 = load_list(offs4, "idx4")
-        pages.append(load_page(1))
+        pages = [load_page(0)]
         idx = load_list(offs, "idx")
-        tab_sb = [load_words(tab_words[0], T, "tab_sb0")]
-        pages.append(load_page(2))
         for q in range(4):
             nc.sync.dma_start(
                 tab_plane[32 * q : 32 * q + 8, :].bitcast(I32),
                 tab_scales[:, 4 * q : 4 * q + 4, :].bitcast(I32),
             )
-        tab_sb.append(load_words(tab_words[1], T, "tab_sb1"))
+        pages.append(load_page(1))
+        tab_sb = held([P, 2, T], U32, "tab_sb")
+        load_words(tab_sb[:, 0, :], tab_words[0])
+        pages.append(load_page(2))
+        load_words(tab_sb[:, 1, :], tab_words[1])
         pages.append(load_page(3))
-        w1_raw = {}
-        for a in range(2):
-            w1_raw[a, 0] = load_rows(w1, a, slice(0, PASS), "stage%d" % a)
-        pages.append(load_page(4))
         wg1_sb = load_gain(wg1, "wg1_sb")
-        wf_sb = load_channel_weights(wf, "wf_sb")
-        idx3 = load_list(offs3, "idx3")
+        wf_rows = load_channel_weights(wf, "wf_rows", nc.sync)
+        pages.append(load_page(4))
+        w1_raw = {(0, 0): load_w1(0, 0)}
         pages.append(load_page(5))
+        w1_raw[1, 0] = load_w1(1, 0)
         pages.append(load_page(6))
-        for a in range(2):
-            w1_raw[a, 1] = load_rows(w1, a, slice(PASS, H), "stage%d" % (2 + a))
+        pages.append(load_page(7))
+        idx3 = load_list(offs3, "idx3")
         idx5 = load_list(offs5, "idx5")
-        base_sb = {}
-        for c in range(1, len(CHUNKS)):
-            m0, width = CHUNKS[c]
-            for b in range(2):
-                base_sb[c, b] = load_rows(base, b, slice(m0, m0 + width), "base%d_%d" % (c, b))
+        w1_raw[0, 1] = load_w1(0, 1)
+        w1_raw[1, 1] = load_w1(1, 1)
 
-        w2_codes = keep.tile([P, 2 * H], U8, name="w2_codes", align_bytes=64)
-        w2_sc = keep.tile([P, H], U8, name="w2_sc", align_bytes=64)
+        w2_codes = held([P, 2 * H], U8, "tab2_sb")
+        w2_sc = held([P, H], U8, "w2_sc")
 
-        def deal_w2_codes(b):
-            cols = slice(2 * b * PASS, 2 * (b + 1) * PASS)
-            nc.vector.tensor_copy(
-                w2_codes[:, cols].rearrange("p (t m e) -> p t m e", t=PACK, e=2),
-                w2_raw[:, cols].rearrange("p (m t e) -> p t m e", t=PACK, e=2),
-            )
+        def deal_w2(slots):
+            for dst, src in ((w2_codes, w2_raw), (w2_sc, w2_plane)):
+                nc.vector.tensor_copy(
+                    dst[:].bitcast(I32).rearrange("p (b t q e) -> p b t q e", b=2, t=PACK, q=16)[:, :, slots],
+                    src[:].bitcast(I32).rearrange("p (b q t e) -> p b t q e", b=2, t=PACK, q=16)[:, :, slots],
+                )
 
-        def deal_w2_scales(b):
-            cols = slice(b * PASS, (b + 1) * PASS)
-            nc.vector.tensor_copy(
-                w2_sc[:, cols].rearrange("p (t m) -> p t m", t=PACK),
-                w2_plane[:, cols].rearrange("p (m t) -> p t m", t=PACK),
-            )
-
-        deal_w2_codes(0)
-        v2_codes = gather(tab2_sb, idx2, U32, "v2_codes")
-        v2_sc = gather(tab2_plane, idx2, U8, "v2_sc")
-        deal_w2_scales(0)
-        deal_w2_codes(1)
-        deal_w2_scales(1)
+        v2_codes = gather(tab2_sb[:], idx2, U32, "v2_codes")
+        v2_sc = gather(tab2_plane[:], idx2, U8, "v2_sc")
+        deal_w2(slice(0, 1))
+        deal_w2(slice(1, PACK))
         wg2_turned = turn_gain(wg2_sb)
+        wp_sb = turn_channel_weights(wp_rows, "wp_sb")
         wg2_rep = {}
-        pres_ops = {}
 
-        def pressure_operands(i):
+        def slot(tag):
+            return held([P, S], F32, tag)[:]
+
+        def pressure_gain(i, gain):
             t = i % PACK
-            ops = operands(i)
-            bank = psum.tile([P, S], F32, name="bank", bufs=7)
+            if t not in wg2_rep:
+                wg2_rep[t] = repeat_gain(wg2_turned, t, room[:, t, :])
+            scaled_gain(wg2_rep[t], wp_sb, i, gain)
+            return gain
+
+        def pressure_root(i, root, square):
+            bank = new_bank()
             nc.tensor.matmul_mx(
                 out=bank[:],
                 lhsT=w2_codes[:, 2 * i * P : 2 * (i + 1) * P].bitcast(FP4X4),
@@ -221,117 +234,176 @@ def tile_list_membrane_fouling_slots_kernel(
                 start=True,
                 stop=True,
             )
-            if t not in wg2_rep:
-                wg2_rep[t] = repeat_gain(wg2_turned, t)
-            scaled_gain(wg2_rep[t], wp_sb, i, ops[:, 0, :])
-            nc.scalar.activation(ops[:, 1, :], bank[:], ACT.Square, bias=zero_root[:])
-            nc.scalar.activation(ops[:, 1, :], ops[:, 1, :], ACT.Sqrt, bias=1.0)
-            pres_ops[i] = ops
+            nc.scalar.activation(square, bank[:], ACT.Square, bias=zero_root[:])
+            nc.scalar.activation(root, square, ACT.Sqrt, bias=1.0)
+            return root
 
-        def scatter(i, lst, ops):
-            nc.vector.tensor_tensor(pages[i][:].indirect(lst[:]), ops[:, 1, :], ops[:, 0, :], ALU.mult)
+        def pressure(i, square=None, root=None):
+            gain = pressure_gain(i, slot("gain%d" % i))
+            if root is None:
+                root = slot("root%d" % i)
+            scatter(i, idx4, gain, pressure_root(i, root, root if square is None else square))
 
+        v_sc = gather(tab_plane[:], idx, U8, "v_sc")
+        room = held([P, 1, S], F32, "first_repeat")
+        pressure(0, square=slot("repeats"))
+        wg2_rep.clear()
+        room = held([P, PACK + 2, S], F32, "repeats")
+        pressure(1, root=room[:, PACK, :])
+        v_codes = [gather(tab_sb[:, 0, :], idx, U32, "gain1")]
+        pressure(2, root=room[:, PACK + 1, :])
+        v_codes.append(gather(tab_sb[:, 1, :], idx, U32, "gain2"))
+        pressure(3)
+        pressure(4)
+        pressure(5, square=slot("grouped0"))
         w1_q = {}
 
-        def quantize_w1(a, b):
-            w1_q[a, b] = quantize(interleave_dealt(w1_raw[a, b]), keep, "w1_%d%d" % (a, b))
+        def quantize_w1(b, tag):
+            grouped = held([P, 2 * PACK * PASS], BF16, "grouped%d" % b)
+            for a in range(2):
+                interleave_dealt(grouped[:, a * PACK * PASS : (a + 1) * PACK * PASS], w1_raw[a, b][:])
+            w1_q[b] = quantize(grouped[:], tag, "w1_sc%d" % b)
 
-        for i in range(2):
-            pressure_operands(i)
-            scatter(i, idx4, pres_ops[i])
-        v_codes = [gather(tab_sb[0], idx, U32, "v_codes0")]
-        pressure_operands(2)
-        scatter(2, idx4, pres_ops[2])
-        v_sc = gather(tab_plane, idx, U8, "v_sc")
-        v_codes.append(gather(tab_sb[1], idx, U32, "v_codes1"))
-        for i in range(3, 6):
-            pressure_operands(i)
-            scatter(i, idx4, pres_ops[i])
-        for a in range(2):
-            quantize_w1(a, 0)
-        pressure_operands(6)
-        scatter(6, idx4, pres_ops[6])
-        pressure_operands(LAST)
+        quantize_w1(0, "gain5")
+        squares = held([P, 2, S], F32, "late_room")
+        pressure(6, square=squares[:, 0, :])
+        last_ops = held([P, 2, S], F32, "grouped1")
+        pressure_gain(LAST, last_ops[:, 0, :])
+        pressure_root(LAST, last_ops[:, 1, :], squares[:, 1, :])
+        scatter(LAST, idx4, last_ops[:, 0, :], last_ops[:, 1, :])
 
         wg1_turned = turn_gain(wg1_sb)
+        wf_sb = turn_channel_weights(wf_rows, "wf_sb")
         wg1_rep = {}
+        room = held([P, PACK, S], F32, "repeats")
 
-        def feed_operands(i):
+        def feed(i, gain, h):
             b, t = divmod(i, PACK)
-            ops = operands(i)
-            bank = psum.tile([P, S], F32, name="bank", bufs=7)
+            if t not in wg1_rep:
+                wg1_rep[t] = repeat_gain(wg1_turned, t, room[:, t, :])
+            scaled_gain(wg1_rep[t], wf_sb, i, gain)
+            bank = new_bank()
             for a in range(2):
-                codes, scales = w1_q[a, b]
+                codes, scales = w1_q[b]
+                cols = slice(a * PASS + t * P, a * PASS + (t + 1) * P)
                 nc.tensor.matmul_mx(
                     out=bank[:],
-                    lhsT=codes[:, t * P : (t + 1) * P].bitcast(FP8X4),
-                    lhsT_scale=scales[:, t * P : (t + 1) * P],
+                    lhsT=codes[:, cols].bitcast(FP8X4),
+                    lhsT_scale=scales[:, cols],
                     rhs=v_codes[a][:].bitcast(FP8X4),
                     rhs_scale=v_sc[4 * a : P, :],
                     start=(a == 0),
                     stop=(a == 1),
                 )
-            if t not in wg1_rep:
-                wg1_rep[t] = repeat_gain(wg1_turned, t)
-            scaled_gain(wg1_rep[t], wf_sb, i, ops[:, 0, :])
-            nc.scalar.activation(ops[:, 1, :], bank[:], ACT.Sigmoid)
-            return ops
+            nc.scalar.activation(h, bank[:], ACT.Sigmoid)
+            scatter(i, idx3, gain, h)
 
-        for i in range(PACK):
-            scatter(i, idx3, feed_operands(i))
+        first_h = held([P, PACK, S], F32, "late_room")
+        feed(0, slot("grouped0"), first_h[:, 0, :])
+        feed(1, slot("feed_gain1"), first_h[:, 1, :])
+        quantize_w1(1, "gain6")
+        feed(2, slot("stage2"), first_h[:, 2, :])
+        feed(3, slot("stage3"), first_h[:, 3, :])
+        w3_raw = held([P, 2, PACK, N], F32, "tab_sb")
         for b in range(2):
-            base_sb[0, b] = load_rows(base, b, slice(0, CHUNKS[0][1]), "stage%d" % b)
-        for a in range(2):
-            quantize_w1(a, 1)
-        w3_raw = [load_rows(w3, b, slice(0, N), "stage%d" % (2 + b)) for b in range(2)]
-        pages.append(load_page(LAST))
-        for i in range(PACK, LAST):
-            scatter(i, idx3, feed_operands(i))
-        last_feed = feed_operands(LAST)
-        w3_q = [quantize(interleave(w3_raw[b]), keep, "w3_%d" % b) for b in range(2)]
-        scatter(LAST, idx4, pres_ops[LAST])
-        scatter(LAST, idx3, last_feed)
+            for t in range(PACK):
+                nc.sync.dma_start(w3_raw[:, b, t, :], slot_rows(w3, b, t))
+        base_sb = [[load_base(b, u) for u in range(2)] for b in range(2)]
+        for i in range(PACK, ROW_TILES):
+            feed(i, slot("feed_gain%d" % i), slot("root%d" % (i - 1)))
 
-        def pick(c, b):
-            m0, width = CHUNKS[c]
-            picked = ring.tile([P, PACK, width], F32, name="picked", tag="picked")
+        w3_grouped = held([P, 2 * PACK * N], BF16, "grouped0")
+        for b in range(2):
+            interleave(nc.scalar.copy, w3_grouped[:, b * PACK * N : (b + 1) * PACK * N], w3_raw[:, b, :, :])
+        w3_codes, w3_sc = quantize(w3_grouped[:], "w3_codes", "w3_sc")
+
+        def pick(b, m0, width, tag):
+            picked = held([P, PACK, width], F32, tag)
             lst = idx5[:, m0 // 16 : (m0 + width) // 16]
             for t in range(PACK):
                 nc.vector.tensor_tensor(
-                    picked[:, t, :], pages[PACK * b + t][:].indirect(lst), base_sb[c, b][:, t, :], ALU.subtract
+                    picked[:, t, :],
+                    pages[PACK * b + t][:].indirect(lst),
+                    base_sb[b][t // 2][:, t % 2, m0 : m0 + width],
+                    ALU.subtract,
                 )
-            return interleave(picked)
+            return picked
 
         out_rows = out.rearrange("(n p) m -> p n m", p=P)
+
+        def product(bank, n, b, x_q, cols):
+            w3_cols = slice(b * N + n * P, b * N + (n + 1) * P)
+            nc.tensor.matmul_mx(
+                out=bank,
+                lhsT=w3_codes[:, w3_cols].bitcast(FP8X4),
+                lhsT_scale=w3_sc[:, w3_cols],
+                rhs=x_q[0][:, cols].bitcast(FP8X4),
+                rhs_scale=x_q[1][:, cols],
+                start=(b == 0),
+                stop=(b == 1),
+            )
+
         banks = {}
 
-        def multiply(c, b, grouped):
+        def open_chunk(c, x_q, x0):
             m0, width = CHUNKS[c]
-            x_codes, x_scales = quantize(grouped, ring, "x")
-            codes, scales = w3_q[b]
+            banks[c] = [new_bank(width) for n in range(N // P)]
             for n in range(N // P):
-                if b == 0:
-                    banks[n] = psum.tile([P, width], F32, name="bank", bufs=7)
-                nc.tensor.matmul_mx(
-                    out=banks[n][:],
-                    lhsT=codes[:, n * P : (n + 1) * P].bitcast(FP8X4),
-                    lhsT_scale=scales[:, n * P : (n + 1) * P],
-                    rhs=x_codes[:].bitcast(FP8X4),
-                    rhs_scale=x_scales[:],
-                    start=(b == 0),
-                    stop=(b == 1),
-                )
-            if b == 1:
-                tag = "stage0" if c == 0 else "base%d_0" % c
-                result = keep.tile([P, N // P, width], F32, name="result", tag=tag)
-                for n in range(N // P):
-                    nc.scalar.copy(result[:, n, :], banks[n][:])
+                product(banks[c][n][:], n, 0, x_q, slice(m0 - x0, m0 - x0 + width))
+
+        def close_chunk(c, x_q):
+            m0, width = CHUNKS[c]
+            if c > 0:
+                result = held([P, N // P, width], F32, "page%d" % c)
+            for n in range(N // P):
+                product(banks[c][n][:], n, 1, x_q, slice(0, width))
+                if c == 0:
+                    rows = held([P, width], F32, "feed_gain%d" % (PACK + n))
+                    nc.scalar.copy(rows[:], banks[c][n][:])
+                    nc.sync.dma_start(out_rows[:, n, m0 : m0 + width], rows[:])
+                else:
+                    copy = nc.vector.tensor_copy if c == len(CHUNKS) - 1 and n % 2 else nc.scalar.copy
+                    copy(result[:, n, :], banks[c][n][:])
+            if c > 0:
                 nc.sync.dma_start(out_rows[:, :, m0 : m0 + width], result[:])
 
-        units = [(c, b) for c in range(len(CHUNKS)) for b in range(2)]
-        waiting = pick(*units[0])
-        for u in range(1, len(units)):
-            picked_next = pick(*units[u])
-            multiply(*units[u - 1], waiting)
-            waiting = picked_next
-        multiply(*units[-1], waiting)
+        units = [(0, 0, PASS), (1, 0, PASS), (0, PASS, PASS)] + [(1,) + chunk for chunk in CHUNKS[1:]]
+        rooms3 = ("grouped1", "grouped0", "tab_sb")
+
+        def round_unit(u):
+            b, m0, width = units[u]
+            picked = pick(b, m0, width, rooms3[u % 3])
+            grouped = held([P, PACK * width], BF16, rooms3[(u + 2) % 3])[:]
+            return picked, grouped
+
+        def quantize_unit(u, grouped):
+            return quantize(grouped, "x_codes%d" % u, "x_sc%d" % u)
+
+        def finish(u, grouped):
+            x_q = quantize_unit(u, grouped)
+            if u == 0:
+                open_chunk(0, x_q, 0)
+            elif u == 1:
+                close_chunk(0, x_q)
+            elif u == 2:
+                upper.append(x_q)
+                open_chunk(1, x_q, PASS)
+                open_chunk(3, x_q, PASS)
+            else:
+                if u == 4:
+                    open_chunk(2, upper[0], PASS)
+                close_chunk(u - 2, x_q)
+
+        upper = []
+        waiting = None
+        for u in range(len(units)):
+            picked, grouped = round_unit(u)
+            if u == len(units) - 1:
+                finish(u - 1, waiting)
+                interleave(nc.vector.tensor_copy, grouped, picked[:])
+            else:
+                interleave(nc.scalar.copy, grouped, picked[:])
+                if u > 0:
+                    finish(u - 1, waiting)
+            waiting = grouped
+        finish(len(units) - 1, waiting)

@@ -57,33 +57,18 @@ def tile_list_membrane_fouling_slots_kernel(
                 )
             return plane
 
-        def load_channel_weights(src, name, queue):
-            rows = keep.tile([P, P], F32, name=name)
-            nc.gpsimd.memset(rows[:], 0.0)
-            for b in range(2):
-                queue.dma_start(
-                    rows[PACK * b : PACK * (b + 1), :].rearrange("t (q j) -> t q j", j=8),
-                    src[b * PASS : (b + 1) * PASS].rearrange("(q t j) -> t q j", t=PACK, j=8),
-                )
-            return rows
-
-        def turn_channel_weights(rows, name):
-            bank = new_bank(P)
-            nc.tensor.transpose(bank[:], rows[:], ident[:])
-            columns = keep.tile([P, ROW_TILES], F32, name=name)
-            nc.scalar.copy(columns[:], bank[:, :ROW_TILES])
-            return columns
+        def load_channel_weights(src, name):
+            vec = keep.tile([P, H // PASS, PACK], F32, name=name)
+            nc.sync.dma_start(vec[:], src.rearrange("(b p t) -> p b t", p=P, t=PACK))
+            return vec
 
         def pass_rows(src, g):
             return src[g * PASS : (g + 1) * PASS, :].rearrange("(p t) c -> p t c", t=PACK)
 
-        def slot_rows(src, b, t):
-            return src[b * PASS : (b + 1) * PASS, :].rearrange("(q t j) c -> t q j c", t=PACK, j=8)[t]
-
         def load_page(i):
             b, t = divmod(i, PACK)
             page = held([P, T2], F32, "page%d" % i)
-            nc.sync.dma_start(page[:], slot_rows(page0, b, t))
+            nc.sync.dma_start(page[:], pass_rows(page0, b)[:, t, :])
             return page
 
         def load_w1(a, b):
@@ -93,8 +78,7 @@ def tile_list_membrane_fouling_slots_kernel(
 
         def load_base(b, u):
             rows = held([P, 2, M], F32, "stage%d" % (2 * b + u))
-            for e in range(2):
-                nc.sync.dma_start(rows[:, e, :], slot_rows(base, b, 2 * u + e))
+            nc.sync.dma_start(rows[:], pass_rows(base, b)[:, 2 * u : 2 * u + 2, :])
             return rows
 
         def load_gain(src, name):
@@ -122,8 +106,8 @@ def tile_list_membrane_fouling_slots_kernel(
 
         def interleave_dealt(grouped, raw):
             nc.scalar.copy(
-                grouped.rearrange("p (t q j a) -> p q t a j", t=PACK, j=8, a=PACK),
-                raw.rearrange("p a (q t j) -> p q t a j", t=PACK, j=8),
+                grouped.rearrange("p (t m j) -> p m j t", t=PACK, j=PACK),
+                raw.rearrange("p j (m t) -> p m j t", t=PACK),
             )
 
         def turn_gain(gain):
@@ -133,42 +117,41 @@ def tile_list_membrane_fouling_slots_kernel(
             return bank
 
         def repeat_gain(bank, t, rep):
-            rows = bank[:].rearrange("p (c q t j) -> p c t q j", c=S // P, t=PACK, j=8)[:, :, t : t + 1]
-            rep = rep.rearrange("p (c r q j) -> p c r q j", c=S // P, r=4, q=4)
-            nc.scalar.copy(rep, rows.to_broadcast([P, S // P, 4, 4, 8]))
+            rows = bank[:].rearrange("p (c a t) -> p c t a", c=S // P, t=PACK)[:, :, t : t + 1, :]
+            rep = rep.rearrange("p (c r a) -> p c r a", c=S // P, r=4)
+            nc.scalar.copy(rep, rows.to_broadcast([P, S // P, 4, 32]))
             return rep
 
         def scaled_gain(rep, weights, i, gain):
             bank = new_bank()
             for c in range(S // P):
                 nc.tensor.transpose(
-                    bank[:, c * P : (c + 1) * P], rep[:, c].rearrange("p r q j -> p (r q j)"), ident[:]
+                    bank[:, c * P : (c + 1) * P], rep[:, c].rearrange("p r a -> p (r a)"), ident[:]
                 )
-            nc.scalar.activation(gain, bank[:], ACT.Copy, scale=weights[:, i : i + 1])
+            nc.scalar.activation(gain, bank[:], ACT.Copy, scale=weights[:, i // PACK, i % PACK : i % PACK + 1])
 
         def scatter(i, lst, gain, h):
             nc.vector.tensor_tensor(pages[i][:].indirect(lst[:]), h, gain, ALU.mult)
 
 
-        wp_rows = load_channel_weights(wp, "wp_rows", nc.gpsimd)
+        tab_plane = held([P, T], U8, "tab_plane")
+        nc.gpsimd.memset(tab_plane[:].bitcast(I32), 0)
         ident = keep.tile([P, P], F32, name="ident")
         make_identity(nc, ident[:])
         zero = keep.tile([P, 1], F32, name="zero")
         zero_root = keep.tile([P, 1], F32, name="zero_root")
         nc.vector.memset(zero[:], 0.0)
         nc.scalar.activation(zero_root[:], zero[:], ACT.Sqrt)
-        tab_plane = held([P, T], U8, "tab_plane")
-        nc.vector.memset(tab_plane[:].bitcast(I32), 0)
 
-        tab2_sb = held([P, TB], U32, "tab2_sb")
-        load_words(tab2_sb[:], tab2_words[0])
         idx2 = load_list(offs2, "idx2")
         tab2_plane = load_scale_rows(tab2_scales[0], TB, "tab2_plane")
+        wg2_sb = load_gain(wg2, "wg2_sb")
         w2_raw = keep.tile([P, 2 * H], U8, name="w2_raw")
         nc.sync.dma_start(w2_raw[:].bitcast(I32), w2_words[0].bitcast(I32))
-        wg2_sb = load_gain(wg2, "wg2_sb")
+        tab2_sb = held([P, TB], U32, "tab2_sb")
+        load_words(tab2_sb[:], tab2_words[0])
         w2_plane = load_scale_rows(w2_scales[0], H, "w2_plane")
-        idx4 = load_list(offs4, "idx4")
+        wp_sb = load_channel_weights(wp, "wp_sb")
         pages = [load_page(0)]
         idx = load_list(offs, "idx")
         for q in range(4):
@@ -176,6 +159,7 @@ def tile_list_membrane_fouling_slots_kernel(
                 tab_plane[32 * q : 32 * q + 8, :].bitcast(I32),
                 tab_scales[:, 4 * q : 4 * q + 4, :].bitcast(I32),
             )
+        idx4 = load_list(offs4, "idx4")
         pages.append(load_page(1))
         tab_sb = held([P, 2, T], U32, "tab_sb")
         load_words(tab_sb[:, 0, :], tab_words[0])
@@ -183,7 +167,7 @@ def tile_list_membrane_fouling_slots_kernel(
         load_words(tab_sb[:, 1, :], tab_words[1])
         pages.append(load_page(3))
         wg1_sb = load_gain(wg1, "wg1_sb")
-        wf_rows = load_channel_weights(wf, "wf_rows", nc.sync)
+        wf_sb = load_channel_weights(wf, "wf_sb")
         pages.append(load_page(4))
         w1_raw = {(0, 0): load_w1(0, 0)}
         pages.append(load_page(5))
@@ -195,22 +179,21 @@ def tile_list_membrane_fouling_slots_kernel(
         w1_raw[0, 1] = load_w1(0, 1)
         w1_raw[1, 1] = load_w1(1, 1)
 
-        w2_codes = held([P, 2 * H], U8, "tab2_sb")
-        w2_sc = held([P, H], U8, "w2_sc")
+        w2_codes = held([P, 2 * H], U8, "w2_codes")
 
-        def deal_w2(slots):
-            for dst, src in ((w2_codes, w2_raw), (w2_sc, w2_plane)):
-                nc.vector.tensor_copy(
-                    dst[:].bitcast(I32).rearrange("p (b t q e) -> p b t q e", b=2, t=PACK, q=16)[:, :, slots],
-                    src[:].bitcast(I32).rearrange("p (b q t e) -> p b t q e", b=2, t=PACK, q=16)[:, :, slots],
-                )
+        def deal(dst, src, slots):
+            nc.vector.tensor_copy(
+                dst.rearrange("p (b t m) -> p b t m", b=2, t=PACK)[:, :, slots],
+                src.rearrange("p (b m t) -> p b t m", b=2, t=PACK)[:, :, slots],
+            )
 
-        v2_codes = gather(tab2_sb[:], idx2, U32, "v2_codes")
         v2_sc = gather(tab2_plane[:], idx2, U8, "v2_sc")
-        deal_w2(slice(0, 1))
-        deal_w2(slice(1, PACK))
+        deal(w2_codes[:].bitcast(U16), w2_raw[:].bitcast(U16), slice(0, PACK))
+        v2_codes = gather(tab2_sb[:], idx2, U32, "v2_codes")
+        w2_sc = held([P, H], U8, "tab2_sb")
+        deal(w2_sc[:], w2_plane[:], slice(0, 1))
+        deal(w2_sc[:], w2_plane[:], slice(1, PACK))
         wg2_turned = turn_gain(wg2_sb)
-        wp_sb = turn_channel_weights(wp_rows, "wp_sb")
         wg2_rep = {}
 
         def slot(tag):
@@ -238,20 +221,21 @@ def tile_list_membrane_fouling_slots_kernel(
             nc.scalar.activation(root, square, ACT.Sqrt, bias=1.0)
             return root
 
-        def pressure(i, square=None, root=None):
-            gain = pressure_gain(i, slot("gain%d" % i))
-            if root is None:
-                root = slot("root%d" % i)
+        def pressure(i, square=None, gain=None):
+            gain = pressure_gain(i, slot("gain%d" % i) if gain is None else gain)
+            root = slot("root%d" % i)
             scatter(i, idx4, gain, pressure_root(i, root, root if square is None else square))
 
         v_sc = gather(tab_plane[:], idx, U8, "v_sc")
-        room = held([P, 1, S], F32, "first_repeat")
+        room = held([P, 2, S], F32, "first_repeats")
         pressure(0, square=slot("repeats"))
+        early = room
+        room = held([P, PACK + 3, S], F32, "repeats")
+        wg2_rep[1] = repeat_gain(wg2_turned, 1, early[:, 1, :])
+        pressure(1, square=room[:, PACK, :], gain=room[:, PACK + 2, :])
         wg2_rep.clear()
-        room = held([P, PACK + 2, S], F32, "repeats")
-        pressure(1, root=room[:, PACK, :])
-        v_codes = [gather(tab_sb[:, 0, :], idx, U32, "gain1")]
-        pressure(2, root=room[:, PACK + 1, :])
+        v_codes = [gather(tab_sb[:, 0, :], idx, U32, "root1")]
+        pressure(2, square=room[:, PACK + 1, :])
         v_codes.append(gather(tab_sb[:, 1, :], idx, U32, "gain2"))
         pressure(3)
         pressure(4)
@@ -273,7 +257,6 @@ def tile_list_membrane_fouling_slots_kernel(
         scatter(LAST, idx4, last_ops[:, 0, :], last_ops[:, 1, :])
 
         wg1_turned = turn_gain(wg1_sb)
-        wf_sb = turn_channel_weights(wf_rows, "wf_sb")
         wg1_rep = {}
         room = held([P, PACK, S], F32, "repeats")
 
@@ -306,8 +289,7 @@ def tile_list_membrane_fouling_slots_kernel(
         feed(3, slot("stage3"), first_h[:, 3, :])
         w3_raw = held([P, 2, PACK, N], F32, "tab_sb")
         for b in range(2):
-            for t in range(PACK):
-                nc.sync.dma_start(w3_raw[:, b, t, :], slot_rows(w3, b, t))
+            nc.sync.dma_start(w3_raw[:, b, :, :], pass_rows(w3, b))
         base_sb = [[load_base(b, u) for u in range(2)] for b in range(2)]
         for i in range(PACK, ROW_TILES):
             feed(i, slot("feed_gain%d" % i), slot("root%d" % (i - 1)))

@@ -23,6 +23,7 @@ PASS = P * PACK
 ROW_TILES = H // P
 LAST = ROW_TILES - 1
 CHUNKS = ((0, 512), (512, 256), (768, 128), (896, 128))
+STRETCHES = ((0, 512), (512, 256), (768, 256))
 
 
 def tile_list_membrane_fouling_slots_kernel(
@@ -234,9 +235,9 @@ def tile_list_membrane_fouling_slots_kernel(
         wg2_rep[1] = repeat_gain(wg2_turned, 1, early[:, 1, :])
         pressure(1, square=room[:, PACK, :], gain=room[:, PACK + 2, :])
         wg2_rep.clear()
-        v_codes = [gather(tab_sb[:, 0, :], idx, U32, "root1")]
+        v_codes = [gather(tab_sb[:, 0, :], idx, U32, "root0")]
         pressure(2, square=room[:, PACK + 1, :])
-        v_codes.append(gather(tab_sb[:, 1, :], idx, U32, "gain2"))
+        v_codes.append(gather(tab_sb[:, 1, :], idx, U32, "root1"))
         pressure(3)
         pressure(4)
         pressure(5, square=slot("grouped0"))
@@ -248,7 +249,7 @@ def tile_list_membrane_fouling_slots_kernel(
                 interleave_dealt(grouped[:, a * PACK * PASS : (a + 1) * PACK * PASS], w1_raw[a, b][:])
             w1_q[b] = quantize(grouped[:], tag, "w1_sc%d" % b)
 
-        quantize_w1(0, "gain5")
+        quantize_w1(0, "gain4")
         squares = held([P, 2, S], F32, "late_room")
         pressure(6, square=squares[:, 0, :])
         last_ops = held([P, 2, S], F32, "grouped1")
@@ -349,37 +350,25 @@ def tile_list_membrane_fouling_slots_kernel(
             if c > 0:
                 nc.sync.dma_start(out_rows[:, :, m0 : m0 + width], result[:])
 
-        units = [(0, 0, PASS), (1, 0, PASS), (0, PASS, PASS)] + [(1,) + chunk for chunk in CHUNKS[1:]]
-        rooms3 = ("grouped1", "grouped0", "tab_sb")
-
-        def round_unit(u):
-            b, m0, width = units[u]
-            picked = pick(b, m0, width, rooms3[u % 3])
-            grouped = held([P, PACK * width], BF16, rooms3[(u + 2) % 3])[:]
-            return picked, grouped
-
-        def quantize_unit(u, grouped):
-            return quantize(grouped, "x_codes%d" % u, "x_sc%d" % u)
+        units = []
+        for m0, width in STRETCHES:
+            units.append((0, m0, width))
+            units.extend((1,) + chunk for chunk in CHUNKS if m0 <= chunk[0] < m0 + width)
 
         def finish(u, grouped):
-            x_q = quantize_unit(u, grouped)
-            if u == 0:
-                open_chunk(0, x_q, 0)
-            elif u == 1:
-                close_chunk(0, x_q)
-            elif u == 2:
-                upper.append(x_q)
-                open_chunk(1, x_q, PASS)
-                open_chunk(3, x_q, PASS)
-            else:
-                if u == 4:
-                    open_chunk(2, upper[0], PASS)
-                close_chunk(u - 2, x_q)
+            b, m0, width = units[u]
+            x_q = quantize(grouped, "x_codes%d" % u, "x_sc%d" % u)
+            for c, chunk in enumerate(CHUNKS):
+                if m0 <= chunk[0] < m0 + width:
+                    if b == 0:
+                        open_chunk(c, x_q, m0)
+                    else:
+                        close_chunk(c, x_q)
 
-        upper = []
         waiting = None
-        for u in range(len(units)):
-            picked, grouped = round_unit(u)
+        for u, (b, m0, width) in enumerate(units):
+            picked = pick(b, m0, width, ("late_room", "grouped1")[u % 2])
+            grouped = held([P, PACK * width], BF16, ("repeats", "tab_sb")[u % 2])[:]
             if u == len(units) - 1:
                 finish(u - 1, waiting)
                 interleave(nc.vector.tensor_copy, grouped, picked[:])

@@ -20,8 +20,12 @@ ALU = mybir.AluOpType
 P = 128
 PACK = 4
 PASS = P * PACK
+PASSES = H // PASS
+QUADRANTS = 4
 ROW_TILES = H // P
 LAST = ROW_TILES - 1
+PSUM_BANKS = 8
+LIST_ROWS = 16
 CHUNKS = ((0, 512), (512, 256), (768, 128), (896, 128))
 STRETCHES = ((0, 512), (512, 256), (768, 256))
 
@@ -38,8 +42,11 @@ def tile_list_membrane_fouling_slots_kernel(
         def held(shape, dtype, tag):
             return keep.tile(shape, dtype, name=tag, tag=tag, align_bytes=64)
 
+        def operand(tag):
+            return held([P, S], F32, tag)[:]
+
         def new_bank(width=S):
-            return psum.tile([P, width], F32, name="bank", bufs=8)
+            return psum.tile([P, width], F32, name="bank", bufs=PSUM_BANKS)
 
         def load_list(src, name):
             lst = keep.tile(list(src.shape), U16, name=name)
@@ -49,9 +56,9 @@ def tile_list_membrane_fouling_slots_kernel(
         def load_words(dst, src):
             nc.sync.dma_start(dst.bitcast(I32), src.rearrange("p t i -> p (t i)").bitcast(I32))
 
-        def load_scale_rows(src, width, name):
+        def load_plane(src, width, name):
             plane = held([P, width], U8, name)
-            for q in range(4):
+            for q in range(QUADRANTS):
                 nc.sync.dma_start(
                     plane[32 * q : 32 * q + 32, :].bitcast(I32),
                     src[4 * q : 4 * q + 4, :].bitcast(I32).partition_broadcast(8),
@@ -59,7 +66,7 @@ def tile_list_membrane_fouling_slots_kernel(
             return plane
 
         def load_channel_weights(src, name):
-            vec = keep.tile([P, H // PASS, PACK], F32, name=name)
+            vec = keep.tile([P, PASSES, PACK], F32, name=name)
             nc.sync.dma_start(vec[:], src.rearrange("(b p t) -> p b t", p=P, t=PACK))
             return vec
 
@@ -72,8 +79,8 @@ def tile_list_membrane_fouling_slots_kernel(
             nc.sync.dma_start(page[:], pass_rows(page0, b)[:, t, :])
             return page
 
-        def load_w1(a, b):
-            raw = held([P, PACK, PASS], F32, "late_room" if (a, b) == (1, 0) else "stage%d" % (2 * b + a))
+        def load_w1(a, b, tag):
+            raw = held([P, PACK, PASS], F32, tag)
             nc.sync.dma_start(raw[:], pass_rows(w1, a)[:, :, b * PASS : (b + 1) * PASS])
             return raw
 
@@ -83,14 +90,20 @@ def tile_list_membrane_fouling_slots_kernel(
             return rows
 
         def load_gain(src, name):
-            gain = keep.tile([P, S], F32, name=name)
-            nc.sync.dma_start(gain[:], src)
-            return gain
+            wg = keep.tile([P, S], F32, name=name)
+            nc.sync.dma_start(wg[:], src)
+            return wg
 
         def gather(window, lst, dtype, tag):
-            picked = held([P, S], dtype, tag)
-            nc.vector.tensor_copy(picked[:], window.indirect(lst[:]))
-            return picked
+            gathered = held([P, S], dtype, tag)
+            nc.vector.tensor_copy(gathered[:], window.indirect(lst[:]))
+            return gathered
+
+        def deal(dst, src, slots):
+            nc.vector.tensor_copy(
+                dst.rearrange("p (b t m) -> p b t m", b=PASSES, t=PACK)[:, :, slots],
+                src.rearrange("p (b m t) -> p b t m", b=PASSES, t=PACK)[:, :, slots],
+            )
 
         def quantize(grouped, codes_tag, scales_tag):
             width = grouped.shape[1] // PACK
@@ -111,29 +124,29 @@ def tile_list_membrane_fouling_slots_kernel(
                 raw.rearrange("p j (m t) -> p m j t", t=PACK),
             )
 
-        def turn_gain(gain):
+        def turn_gain(wg):
             bank = new_bank()
             for c in range(S // P):
-                nc.tensor.transpose(bank[:, c * P : (c + 1) * P], gain[:, c * P : (c + 1) * P], ident[:])
+                nc.tensor.transpose(bank[:, c * P : (c + 1) * P], wg[:, c * P : (c + 1) * P], ident[:])
             return bank
 
-        def repeat_gain(bank, t, rep):
-            rows = bank[:].rearrange("p (c a t) -> p c t a", c=S // P, t=PACK)[:, :, t : t + 1, :]
-            rep = rep.rearrange("p (c r a) -> p c r a", c=S // P, r=4)
-            nc.scalar.copy(rep, rows.to_broadcast([P, S // P, 4, 32]))
-            return rep
+        def repeat_gain(turned, t, dst):
+            rows = turned[:].rearrange("p (c a t) -> p c t a", c=S // P, t=PACK)[:, :, t : t + 1, :]
+            repeated = dst.rearrange("p (c r a) -> p c r a", c=S // P, r=PACK)
+            nc.scalar.copy(repeated, rows.to_broadcast([P, S // P, PACK, P // PACK]))
+            return repeated
 
-        def scaled_gain(rep, weights, i, gain):
+        def scaled_gain(repeated, weights, i, gain):
+            b, t = divmod(i, PACK)
             bank = new_bank()
             for c in range(S // P):
                 nc.tensor.transpose(
-                    bank[:, c * P : (c + 1) * P], rep[:, c].rearrange("p r a -> p (r a)"), ident[:]
+                    bank[:, c * P : (c + 1) * P], repeated[:, c].rearrange("p r a -> p (r a)"), ident[:]
                 )
-            nc.scalar.activation(gain, bank[:], ACT.Copy, scale=weights[:, i // PACK, i % PACK : i % PACK + 1])
+            nc.scalar.activation(gain, bank[:], ACT.Copy, scale=weights[:, b, t : t + 1])
 
-        def scatter(i, lst, gain, h):
-            nc.vector.tensor_tensor(pages[i][:].indirect(lst[:]), h, gain, ALU.mult)
-
+        def scatter(i, lst, gain, values):
+            nc.vector.tensor_tensor(pages[i][:].indirect(lst[:]), values, gain, ALU.mult)
 
         tab_plane = held([P, T], U8, "tab_plane")
         nc.gpsimd.memset(tab_plane[:].bitcast(I32), 0)
@@ -145,49 +158,42 @@ def tile_list_membrane_fouling_slots_kernel(
         nc.scalar.activation(zero_root[:], zero[:], ACT.Sqrt)
 
         idx2 = load_list(offs2, "idx2")
-        tab2_plane = load_scale_rows(tab2_scales[0], TB, "tab2_plane")
+        tab2_plane = load_plane(tab2_scales[0], TB, "tab2_plane")
         wg2_sb = load_gain(wg2, "wg2_sb")
         w2_raw = keep.tile([P, 2 * H], U8, name="w2_raw")
         nc.sync.dma_start(w2_raw[:].bitcast(I32), w2_words[0].bitcast(I32))
         tab2_sb = held([P, TB], U32, "tab2_sb")
         load_words(tab2_sb[:], tab2_words[0])
-        w2_plane = load_scale_rows(w2_scales[0], H, "w2_plane")
+        w2_plane = load_plane(w2_scales[0], H, "w2_plane")
         wp_sb = load_channel_weights(wp, "wp_sb")
         pages = [load_page(0)]
         idx = load_list(offs, "idx")
-        for q in range(4):
+        for q in range(QUADRANTS):
             nc.sync.dma_start(
                 tab_plane[32 * q : 32 * q + 8, :].bitcast(I32),
                 tab_scales[:, 4 * q : 4 * q + 4, :].bitcast(I32),
             )
         idx4 = load_list(offs4, "idx4")
         pages.append(load_page(1))
-        tab_sb = held([P, 2, T], U32, "tab_sb")
+        tab_sb = held([P, PASSES, T], U32, "tab_sb")
         load_words(tab_sb[:, 0, :], tab_words[0])
         pages.append(load_page(2))
-        load_words(tab_sb[:, 1, :], tab_words[1])
         pages.append(load_page(3))
         wg1_sb = load_gain(wg1, "wg1_sb")
         wf_sb = load_channel_weights(wf, "wf_sb")
         pages.append(load_page(4))
-        w1_raw = {(0, 0): load_w1(0, 0)}
+        w1_raw = {(0, 0): load_w1(0, 0, "stage0")}
         pages.append(load_page(5))
-        w1_raw[1, 0] = load_w1(1, 0)
+        w1_raw[1, 0] = load_w1(1, 0, "late_room")
+        load_words(tab_sb[:, 1, :], tab_words[1])
         pages.append(load_page(6))
         pages.append(load_page(7))
         idx3 = load_list(offs3, "idx3")
         idx5 = load_list(offs5, "idx5")
-        w1_raw[0, 1] = load_w1(0, 1)
-        w1_raw[1, 1] = load_w1(1, 1)
+        w1_raw[0, 1] = load_w1(0, 1, "stage2")
+        w1_raw[1, 1] = load_w1(1, 1, "stage3")
 
         w2_codes = held([P, 2 * H], U8, "w2_codes")
-
-        def deal(dst, src, slots):
-            nc.vector.tensor_copy(
-                dst.rearrange("p (b t m) -> p b t m", b=2, t=PACK)[:, :, slots],
-                src.rearrange("p (b m t) -> p b t m", b=2, t=PACK)[:, :, slots],
-            )
-
         v2_sc = gather(tab2_plane[:], idx2, U8, "v2_sc")
         deal(w2_codes[:].bitcast(U16), w2_raw[:].bitcast(U16), slice(0, PACK))
         v2_codes = gather(tab2_sb[:], idx2, U32, "v2_codes")
@@ -195,19 +201,18 @@ def tile_list_membrane_fouling_slots_kernel(
         deal(w2_sc[:], w2_plane[:], slice(0, 1))
         deal(w2_sc[:], w2_plane[:], slice(1, PACK))
         wg2_turned = turn_gain(wg2_sb)
-        wg2_rep = {}
 
-        def slot(tag):
-            return held([P, S], F32, tag)[:]
-
-        def pressure_gain(i, gain):
+        def pressure(i, repeats, made, square=None, gain=None, root=None):
             t = i % PACK
-            if t not in wg2_rep:
-                wg2_rep[t] = repeat_gain(wg2_turned, t, room[:, t, :])
-            scaled_gain(wg2_rep[t], wp_sb, i, gain)
-            return gain
-
-        def pressure_root(i, root, square):
+            if gain is None:
+                gain = operand("gain%d" % i)
+            if t not in made:
+                made[t] = repeat_gain(wg2_turned, t, repeats[:, t, :])
+            scaled_gain(made[t], wp_sb, i, gain)
+            if root is None:
+                root = operand("root%d" % i)
+            if square is None:
+                square = root
             bank = new_bank()
             nc.tensor.matmul_mx(
                 out=bank[:],
@@ -220,55 +225,51 @@ def tile_list_membrane_fouling_slots_kernel(
             )
             nc.scalar.activation(square, bank[:], ACT.Square, bias=zero_root[:])
             nc.scalar.activation(root, square, ACT.Sqrt, bias=1.0)
-            return root
+            scatter(i, idx4, gain, root)
 
-        def pressure(i, square=None, gain=None):
-            gain = pressure_gain(i, slot("gain%d" % i) if gain is None else gain)
-            root = slot("root%d" % i)
-            scatter(i, idx4, gain, pressure_root(i, root, root if square is None else square))
-
-        v_sc = gather(tab_plane[:], idx, U8, "v_sc")
-        room = held([P, 2, S], F32, "first_repeats")
-        pressure(0, square=slot("repeats"))
-        early = room
-        room = held([P, PACK + 3, S], F32, "repeats")
-        wg2_rep[1] = repeat_gain(wg2_turned, 1, early[:, 1, :])
-        pressure(1, square=room[:, PACK, :], gain=room[:, PACK + 2, :])
-        wg2_rep.clear()
-        v_codes = [gather(tab_sb[:, 0, :], idx, U32, "root0")]
-        pressure(2, square=room[:, PACK + 1, :])
-        v_codes.append(gather(tab_sb[:, 1, :], idx, U32, "root1"))
-        pressure(3)
-        pressure(4)
-        pressure(5, square=slot("grouped0"))
         w1_q = {}
 
-        def quantize_w1(b, tag):
-            grouped = held([P, 2 * PACK * PASS], BF16, "grouped%d" % b)
-            for a in range(2):
+        def quantize_w1(b, codes_tag):
+            grouped = held([P, PASSES * PACK * PASS], BF16, "grouped%d" % b)
+            for a in range(PASSES):
                 interleave_dealt(grouped[:, a * PACK * PASS : (a + 1) * PACK * PASS], w1_raw[a, b][:])
-            w1_q[b] = quantize(grouped[:], tag, "w1_sc%d" % b)
+            w1_q[b] = quantize(grouped[:], codes_tag, "w1_sc%d" % b)
 
-        quantize_w1(0, "gain4")
-        squares = held([P, 2, S], F32, "late_room")
-        pressure(6, square=squares[:, 0, :])
-        last_ops = held([P, 2, S], F32, "grouped1")
-        pressure_gain(LAST, last_ops[:, 0, :])
-        pressure_root(LAST, last_ops[:, 1, :], squares[:, 1, :])
-        scatter(LAST, idx4, last_ops[:, 0, :], last_ops[:, 1, :])
+        v_sc = gather(tab_plane[:], idx, U8, "v_sc")
+        first_repeats = held([P, 2, S], F32, "first_repeats")
+        made = {}
+        pressure(0, first_repeats, made, square=operand("repeats"))
+        repeats = held([P, PACK + 3, S], F32, "repeats")
+        made[1] = repeat_gain(wg2_turned, 1, first_repeats[:, 1, :])
+        pressure(1, repeats, made, square=repeats[:, PACK, :], gain=repeats[:, PACK + 2, :])
+        made = {}
+        v_codes = [gather(tab_sb[:, 0, :], idx, U32, "root0")]
+        pressure(2, repeats, made, square=repeats[:, PACK + 1, :])
+        pressure(3, repeats, made)
+        pressure(4, repeats, made)
+        pressure(5, repeats, made, square=operand("grouped0"))
+        v_codes.append(gather(tab_sb[:, 1, :], idx, U32, "gain5"))
+        quantize_w1(0, "gain3")
+        last_squares = held([P, 2, S], F32, "late_room")
+        pressure(LAST - 1, repeats, made, square=last_squares[:, 0, :])
+        last_operands = held([P, 2, S], F32, "grouped1")
+        pressure(
+            LAST, repeats, made,
+            square=last_squares[:, 1, :], gain=last_operands[:, 0, :], root=last_operands[:, 1, :],
+        )
 
         wg1_turned = turn_gain(wg1_sb)
-        wg1_rep = {}
-        room = held([P, PACK, S], F32, "repeats")
+        feed_made = {}
+        feed_repeats = held([P, PACK, S], F32, "repeats")
 
-        def feed(i, gain, h):
+        def feed(i, gain, sigmoid):
             b, t = divmod(i, PACK)
-            if t not in wg1_rep:
-                wg1_rep[t] = repeat_gain(wg1_turned, t, room[:, t, :])
-            scaled_gain(wg1_rep[t], wf_sb, i, gain)
+            if t not in feed_made:
+                feed_made[t] = repeat_gain(wg1_turned, t, feed_repeats[:, t, :])
+            scaled_gain(feed_made[t], wf_sb, i, gain)
             bank = new_bank()
-            for a in range(2):
-                codes, scales = w1_q[b]
+            codes, scales = w1_q[b]
+            for a in range(PASSES):
                 cols = slice(a * PASS + t * P, a * PASS + (t + 1) * P)
                 nc.tensor.matmul_mx(
                     out=bank[:],
@@ -277,32 +278,32 @@ def tile_list_membrane_fouling_slots_kernel(
                     rhs=v_codes[a][:].bitcast(FP8X4),
                     rhs_scale=v_sc[4 * a : P, :],
                     start=(a == 0),
-                    stop=(a == 1),
+                    stop=(a == PASSES - 1),
                 )
-            nc.scalar.activation(h, bank[:], ACT.Sigmoid)
-            scatter(i, idx3, gain, h)
+            nc.scalar.activation(sigmoid, bank[:], ACT.Sigmoid)
+            scatter(i, idx3, gain, sigmoid)
 
-        first_h = held([P, PACK, S], F32, "late_room")
-        feed(0, slot("grouped0"), first_h[:, 0, :])
-        feed(1, slot("feed_gain1"), first_h[:, 1, :])
+        first_sigmoids = held([P, PACK, S], F32, "late_room")
+        feed(0, operand("grouped0"), first_sigmoids[:, 0, :])
+        feed(1, operand("feed_gain1"), first_sigmoids[:, 1, :])
         quantize_w1(1, "gain6")
-        feed(2, slot("stage2"), first_h[:, 2, :])
-        feed(3, slot("stage3"), first_h[:, 3, :])
-        w3_raw = held([P, 2, PACK, N], F32, "tab_sb")
-        for b in range(2):
+        feed(2, operand("stage2"), first_sigmoids[:, 2, :])
+        feed(3, operand("stage3"), first_sigmoids[:, 3, :])
+        w3_raw = held([P, PASSES, PACK, N], F32, "tab_sb")
+        for b in range(PASSES):
             nc.sync.dma_start(w3_raw[:, b, :, :], pass_rows(w3, b))
-        base_sb = [[load_base(b, u) for u in range(2)] for b in range(2)]
+        base_sb = [[load_base(b, u) for u in range(2)] for b in range(PASSES)]
         for i in range(PACK, ROW_TILES):
-            feed(i, slot("feed_gain%d" % i), slot("root%d" % (i - 1)))
+            feed(i, operand("feed_gain%d" % i), operand("root%d" % (i - 1)))
 
-        w3_grouped = held([P, 2 * PACK * N], BF16, "grouped0")
-        for b in range(2):
+        w3_grouped = held([P, PASSES * PACK * N], BF16, "grouped0")
+        for b in range(PASSES):
             interleave(nc.scalar.copy, w3_grouped[:, b * PACK * N : (b + 1) * PACK * N], w3_raw[:, b, :, :])
         w3_codes, w3_sc = quantize(w3_grouped[:], "w3_codes", "w3_sc")
 
         def pick(b, m0, width, tag):
             picked = held([P, PACK, width], F32, tag)
-            lst = idx5[:, m0 // 16 : (m0 + width) // 16]
+            lst = idx5[:, m0 // LIST_ROWS : (m0 + width) // LIST_ROWS]
             for t in range(PACK):
                 nc.vector.tensor_tensor(
                     picked[:, t, :],
@@ -312,20 +313,20 @@ def tile_list_membrane_fouling_slots_kernel(
                 )
             return picked
 
-        out_rows = out.rearrange("(n p) m -> p n m", p=P)
-
         def product(bank, n, b, x_q, cols):
+            x_codes, x_sc = x_q
             w3_cols = slice(b * N + n * P, b * N + (n + 1) * P)
             nc.tensor.matmul_mx(
                 out=bank,
                 lhsT=w3_codes[:, w3_cols].bitcast(FP8X4),
                 lhsT_scale=w3_sc[:, w3_cols],
-                rhs=x_q[0][:, cols].bitcast(FP8X4),
-                rhs_scale=x_q[1][:, cols],
+                rhs=x_codes[:, cols].bitcast(FP8X4),
+                rhs_scale=x_sc[:, cols],
                 start=(b == 0),
-                stop=(b == 1),
+                stop=(b == PASSES - 1),
             )
 
+        out_rows = out.rearrange("(n p) m -> p n m", p=P)
         banks = {}
 
         def open_chunk(c, x_q, x0):
@@ -350,13 +351,13 @@ def tile_list_membrane_fouling_slots_kernel(
             if c > 0:
                 nc.sync.dma_start(out_rows[:, :, m0 : m0 + width], result[:])
 
-        units = []
+        pieces = []
         for m0, width in STRETCHES:
-            units.append((0, m0, width))
-            units.extend((1,) + chunk for chunk in CHUNKS if m0 <= chunk[0] < m0 + width)
+            pieces.append((0, m0, width))
+            pieces.extend((1,) + chunk for chunk in CHUNKS if m0 <= chunk[0] < m0 + width)
 
-        def finish(u, grouped):
-            b, m0, width = units[u]
+        def multiply(u, grouped):
+            b, m0, width = pieces[u]
             x_q = quantize(grouped, "x_codes%d" % u, "x_sc%d" % u)
             for c, chunk in enumerate(CHUNKS):
                 if m0 <= chunk[0] < m0 + width:
@@ -366,15 +367,15 @@ def tile_list_membrane_fouling_slots_kernel(
                         close_chunk(c, x_q)
 
         waiting = None
-        for u, (b, m0, width) in enumerate(units):
+        for u, (b, m0, width) in enumerate(pieces):
             picked = pick(b, m0, width, ("late_room", "grouped1")[u % 2])
             grouped = held([P, PACK * width], BF16, ("repeats", "tab_sb")[u % 2])[:]
-            if u == len(units) - 1:
-                finish(u - 1, waiting)
+            if u == len(pieces) - 1:
+                multiply(u - 1, waiting)
                 interleave(nc.vector.tensor_copy, grouped, picked[:])
             else:
                 interleave(nc.scalar.copy, grouped, picked[:])
                 if u > 0:
-                    finish(u - 1, waiting)
+                    multiply(u - 1, waiting)
             waiting = grouped
-        finish(len(units) - 1, waiting)
+        multiply(len(pieces) - 1, waiting)

from contextlib import ExitStack

import concourse.mybir as mybir
from concourse.masks import make_identity

K, KB, T, TB, S, H, T2, N, M = 1024, 512, 2048, 1024, 512, 1024, 2048, 512, 1024
FLOPS = 2 * (K * H * S + KB * H * S + H * N * M)

F32 = mybir.dt.float32
BF16 = mybir.dt.bfloat16
I32 = mybir.dt.int32
U32 = mybir.dt.uint32
U16 = mybir.dt.uint16
U8 = mybir.dt.uint8
FP8X4 = mybir.dt.float8_e4m3fn_x4
FP4X4 = mybir.dt.float4_e2m1fn_x4
ACT = mybir.ActivationFunctionType
ALU = mybir.AluOpType

P = 128
PACK = 4
PASS = P * PACK
PASSES = H // PASS
QUADRANTS = 4
ROW_TILES = H // P
LAST = ROW_TILES - 1
PSUM_BANKS = 8
LIST_ROWS = 16
CHUNKS = ((0, 512), (512, 256), (768, 128), (896, 128))
STRETCHES = ((0, 512), (512, 256), (768, 256))


def tile_list_membrane_fouling_slots_kernel(
    tc, tab_words, tab_scales, tab2_words, tab2_scales, offs, offs2, offs3, offs4, offs5,
    w1, wf, w2_words, w2_scales, wp, wg1, wg2, page0, base, w3, out,
):
    nc = tc.nc
    with ExitStack() as ctx:
        keep = ctx.enter_context(tc.tile_pool(name="keep", bufs=1))
        psum = ctx.enter_context(tc.psum_pool(name="psum", bufs=1))

        def held(shape, dtype, tag):
            return keep.tile(shape, dtype, name=tag, tag=tag, align_bytes=64)

        def operand(tag):
            return held([P, S], F32, tag)[:]

        def new_bank(width=S):
            return psum.tile([P, width], F32, name="bank", bufs=PSUM_BANKS)

        def load_list(src, name):
            lst = keep.tile(list(src.shape), U16, name=name)
            nc.sync.dma_start(lst[:], src)
            return lst

        def load_words(dst, src):
            nc.sync.dma_start(dst.bitcast(I32), src.rearrange("p t i -> p (t i)").bitcast(I32))

        def load_plane(src, width, name):
            plane = held([P, width], U8, name)
            for q in range(QUADRANTS):
                nc.sync.dma_start(
                    plane[32 * q : 32 * q + 32, :].bitcast(I32),
                    src[4 * q : 4 * q + 4, :].bitcast(I32).partition_broadcast(8),
                )
            return plane

        def load_channel_weights(src, name):
            vec = keep.tile([P, PASSES, PACK], F32, name=name)
            nc.sync.dma_start(vec[:], src.rearrange("(b p t) -> p b t", p=P, t=PACK))
            return vec

        def pass_rows(src, g):
            return src[g * PASS : (g + 1) * PASS, :].rearrange("(p t) c -> p t c", t=PACK)

        def load_page(i):
            b, t = divmod(i, PACK)
            page = held([P, T2], F32, "page%d" % i)
            nc.sync.dma_start(page[:], pass_rows(page0, b)[:, t, :])
            return page

        def load_w1(a, b, tag):
            raw = held([P, PACK, PASS], F32, tag)
            nc.sync.dma_start(raw[:], pass_rows(w1, a)[:, :, b * PASS : (b + 1) * PASS])
            return raw

        def load_base(b, u):
            rows = held([P, 2, M], F32, "stage%d" % (2 * b + u))
            nc.sync.dma_start(rows[:], pass_rows(base, b)[:, 2 * u : 2 * u + 2, :])
            return rows

        def load_gain(src, name):
            wg = keep.tile([P, S], F32, name=name)
            nc.sync.dma_start(wg[:], src)
            return wg

        def gather(window, lst, dtype, tag):
            gathered = held([P, S], dtype, tag)
            nc.vector.tensor_copy(gathered[:], window.indirect(lst[:]))
            return gathered

        def deal(dst, src, slots):
            nc.vector.tensor_copy(
                dst.rearrange("p (b t m) -> p b t m", b=PASSES, t=PACK)[:, :, slots],
                src.rearrange("p (b m t) -> p b t m", b=PASSES, t=PACK)[:, :, slots],
            )

        def quantize(grouped, codes_tag, scales_tag):
            width = grouped.shape[1] // PACK
            codes = held([P, width], U32, codes_tag)
            scales = held([P, width], U8, scales_tag)
            nc.vector.quantize_mx(out=codes[:].bitcast(FP8X4), scales=scales[:], in_=grouped)
            return codes, scales

        def interleave(copy, grouped, raw):
            copy(
                grouped.rearrange("p (c i t) -> p c t i", i=4, t=PACK),
                raw.rearrange("p t (c i) -> p c t i", i=4),
            )

        def interleave_dealt(grouped, raw):
            nc.scalar.copy(
                grouped.rearrange("p (t m j) -> p m j t", t=PACK, j=PACK),
                raw.rearrange("p j (m t) -> p m j t", t=PACK),
            )

        def turn_gain(wg):
            bank = new_bank()
            for c in range(S // P):
                nc.tensor.transpose(bank[:, c * P : (c + 1) * P], wg[:, c * P : (c + 1) * P], ident[:])
            return bank

        def repeat_gain(turned, t, dst):
            rows = turned[:].rearrange("p (c a t) -> p c t a", c=S // P, t=PACK)[:, :, t : t + 1, :]
            repeated = dst.rearrange("p (c r a) -> p c r a", c=S // P, r=PACK)
            nc.scalar.copy(repeated, rows.to_broadcast([P, S // P, PACK, P // PACK]))
            return repeated

        def scaled_gain(repeated, weights, i, gain):
            b, t = divmod(i, PACK)
            bank = new_bank()
            for c in range(S // P):
                nc.tensor.transpose(
                    bank[:, c * P : (c + 1) * P], repeated[:, c].rearrange("p r a -> p (r a)"), ident[:]
                )
            nc.scalar.activation(gain, bank[:], ACT.Copy, scale=weights[:, b, t : t + 1])

        def scatter(i, lst, gain, values):
            nc.vector.tensor_tensor(pages[i][:].indirect(lst[:]), values, gain, ALU.mult)

        tab_plane = held([P, T], U8, "tab_plane")
        nc.gpsimd.memset(tab_plane[:].bitcast(I32), 0)
        ident = keep.tile([P, P], F32, name="ident")
        make_identity(nc, ident[:])
        zero = keep.tile([P, 1], F32, name="zero")
        zero_root = keep.tile([P, 1], F32, name="zero_root")
        nc.vector.memset(zero[:], 0.0)
        nc.scalar.activation(zero_root[:], zero[:], ACT.Sqrt)

        idx2 = load_list(offs2, "idx2")
        tab2_plane = load_plane(tab2_scales[0], TB, "tab2_plane")
        wg2_sb = load_gain(wg2, "wg2_sb")
        w2_raw = keep.tile([P, 2 * H], U8, name="w2_raw")
        nc.sync.dma_start(w2_raw[:].bitcast(I32), w2_words[0].bitcast(I32))
        tab2_sb = held([P, TB], U32, "tab2_sb")
        load_words(tab2_sb[:], tab2_words[0])
        w2_plane = load_plane(w2_scales[0], H, "w2_plane")
        wp_sb = load_channel_weights(wp, "wp_sb")
        pages = [load_page(0)]
        idx = load_list(offs, "idx")
        for q in range(QUADRANTS):
            nc.sync.dma_start(
                tab_plane[32 * q : 32 * q + 8, :].bitcast(I32),
                tab_scales[:, 4 * q : 4 * q + 4, :].bitcast(I32),
            )
        idx4 = load_list(offs4, "idx4")
        pages.append(load_page(1))
        tab_sb = held([P, PASSES, T], U32, "tab_sb")
        load_words(tab_sb[:, 0, :], tab_words[0])
        pages.append(load_page(2))
        pages.append(load_page(3))
        wg1_sb = load_gain(wg1, "wg1_sb")
        wf_sb = load_channel_weights(wf, "wf_sb")
        pages.append(load_page(4))
        w1_raw = {(0, 0): load_w1(0, 0, "stage0")}
        pages.append(load_page(5))
        w1_raw[1, 0] = load_w1(1, 0, "late_room")
        load_words(tab_sb[:, 1, :], tab_words[1])
        pages.append(load_page(6))
        pages.append(load_page(7))
        idx3 = load_list(offs3, "idx3")
        idx5 = load_list(offs5, "idx5")
        w1_raw[0, 1] = load_w1(0, 1, "stage2")
        w1_raw[1, 1] = load_w1(1, 1, "stage3")

        w2_codes = held([P, 2 * H], U8, "w2_codes")
        v2_sc = gather(tab2_plane[:], idx2, U8, "v2_sc")
        deal(w2_codes[:].bitcast(U16), w2_raw[:].bitcast(U16), slice(0, PACK))
        v2_codes = gather(tab2_sb[:], idx2, U32, "v2_codes")
        w2_sc = held([P, H], U8, "tab2_sb")
        deal(w2_sc[:], w2_plane[:], slice(0, 1))
        deal(w2_sc[:], w2_plane[:], slice(1, PACK))
        wg2_turned = turn_gain(wg2_sb)

        def pressure(i, repeats, made, square=None, gain=None, root=None):
            t = i % PACK
            if gain is None:
                gain = operand("gain%d" % i)
            if t not in made:
                made[t] = repeat_gain(wg2_turned, t, repeats[:, t, :])
            scaled_gain(made[t], wp_sb, i, gain)
            if root is None:
                root = operand("root%d" % i)
            if square is None:
                square = root
            bank = new_bank()
            nc.tensor.matmul_mx(
                out=bank[:],
                lhsT=w2_codes[:, 2 * i * P : 2 * (i + 1) * P].bitcast(FP4X4),
                lhsT_scale=w2_sc[:, i * P : (i + 1) * P],
                rhs=v2_codes[:].bitcast(FP8X4),
                rhs_scale=v2_sc[:],
                start=True,
                stop=True,
            )
            nc.scalar.activation(square, bank[:], ACT.Square, bias=zero_root[:])
            nc.scalar.activation(root, square, ACT.Sqrt, bias=1.0)
            scatter(i, idx4, gain, root)

        w1_q = {}

        def quantize_w1(b, codes_tag):
            grouped = held([P, PASSES * PACK * PASS], BF16, "grouped%d" % b)
            for a in range(PASSES):
                interleave_dealt(grouped[:, a * PACK * PASS : (a + 1) * PACK * PASS], w1_raw[a, b][:])
            w1_q[b] = quantize(grouped[:], codes_tag, "w1_sc%d" % b)

        v_sc = gather(tab_plane[:], idx, U8, "v_sc")
        first_repeats = held([P, 2, S], F32, "first_repeats")
        made = {}
        pressure(0, first_repeats, made, square=operand("repeats"))
        repeats = held([P, PACK + 3, S], F32, "repeats")
        made[1] = repeat_gain(wg2_turned, 1, first_repeats[:, 1, :])
        pressure(1, repeats, made, square=repeats[:, PACK, :], gain=repeats[:, PACK + 2, :])
        made = {}
        v_codes = [gather(tab_sb[:, 0, :], idx, U32, "root0")]
        pressure(2, repeats, made, square=repeats[:, PACK + 1, :])
        pressure(3, repeats, made)
        pressure(4, repeats, made)
        pressure(5, repeats, made, square=operand("grouped0"))
        v_codes.append(gather(tab_sb[:, 1, :], idx, U32, "gain5"))
        quantize_w1(0, "gain3")
        last_squares = held([P, 2, S], F32, "late_room")
        pressure(LAST - 1, repeats, made, square=last_squares[:, 0, :])
        last_operands = held([P, 2, S], F32, "grouped1")
        pressure(
            LAST, repeats, made,
            square=last_squares[:, 1, :], gain=last_operands[:, 0, :], root=last_operands[:, 1, :],
        )

        wg1_turned = turn_gain(wg1_sb)
        feed_made = {}
        feed_repeats = held([P, PACK, S], F32, "repeats")

        def feed(i, gain, sigmoid):
            b, t = divmod(i, PACK)
            if t not in feed_made:
                feed_made[t] = repeat_gain(wg1_turned, t, feed_repeats[:, t, :])
            scaled_gain(feed_made[t], wf_sb, i, gain)
            bank = new_bank()
            codes, scales = w1_q[b]
            for a in range(PASSES):
                cols = slice(a * PASS + t * P, a * PASS + (t + 1) * P)
                nc.tensor.matmul_mx(
                    out=bank[:],
                    lhsT=codes[:, cols].bitcast(FP8X4),
                    lhsT_scale=scales[:, cols],
                    rhs=v_codes[a][:].bitcast(FP8X4),
                    rhs_scale=v_sc[4 * a : P, :],
                    start=(a == 0),
                    stop=(a == PASSES - 1),
                )
            nc.scalar.activation(sigmoid, bank[:], ACT.Sigmoid)
            scatter(i, idx3, gain, sigmoid)

        first_sigmoids = held([P, PACK, S], F32, "late_room")
        feed(0, operand("grouped0"), first_sigmoids[:, 0, :])
        feed(1, operand("feed_gain1"), first_sigmoids[:, 1, :])
        quantize_w1(1, "gain6")
        feed(2, operand("stage2"), first_sigmoids[:, 2, :])
        feed(3, operand("stage3"), first_sigmoids[:, 3, :])
        w3_raw = held([P, PASSES, PACK, N], F32, "tab_sb")
        for b in range(PASSES):
            nc.sync.dma_start(w3_raw[:, b, :, :], pass_rows(w3, b))
        base_sb = [[load_base(b, u) for u in range(2)] for b in range(PASSES)]
        for i in range(PACK, ROW_TILES):
            feed(i, operand("feed_gain%d" % i), operand("root%d" % (i - 1)))

        w3_grouped = held([P, PASSES * PACK * N], BF16, "grouped0")
        for b in range(PASSES):
            interleave(nc.scalar.copy, w3_grouped[:, b * PACK * N : (b + 1) * PACK * N], w3_raw[:, b, :, :])
        w3_codes, w3_sc = quantize(w3_grouped[:], "w3_codes", "w3_sc")

        def pick(b, m0, width, tag):
            picked = held([P, PACK, width], F32, tag)
            lst = idx5[:, m0 // LIST_ROWS : (m0 + width) // LIST_ROWS]
            for t in range(PACK):
                nc.vector.tensor_tensor(
                    picked[:, t, :],
                    pages[PACK * b + t][:].indirect(lst),
                    base_sb[b][t // 2][:, t % 2, m0 : m0 + width],
                    ALU.subtract,
                )
            return picked

        def product(bank, n, b, x_q, cols):
            x_codes, x_sc = x_q
            w3_cols = slice(b * N + n * P, b * N + (n + 1) * P)
            nc.tensor.matmul_mx(
                out=bank,
                lhsT=w3_codes[:, w3_cols].bitcast(FP8X4),
                lhsT_scale=w3_sc[:, w3_cols],
                rhs=x_codes[:, cols].bitcast(FP8X4),
                rhs_scale=x_sc[:, cols],
                start=(b == 0),
                stop=(b == PASSES - 1),
            )

        out_rows = out.rearrange("(n p) m -> p n m", p=P)
        banks = {}

        def open_chunk(c, x_q, x0):
            m0, width = CHUNKS[c]
            banks[c] = [new_bank(width) for n in range(N // P)]
            for n in range(N // P):
                product(banks[c][n][:], n, 0, x_q, slice(m0 - x0, m0 - x0 + width))

        def close_chunk(c, x_q):
            m0, width = CHUNKS[c]
            if c > 0:
                result = held([P, N // P, width], F32, "page%d" % c)
            for n in range(N // P):
                product(banks[c][n][:], n, 1, x_q, slice(0, width))
                if c == 0:
                    rows = held([P, width], F32, "feed_gain%d" % (PACK + n))
                    nc.scalar.copy(rows[:], banks[c][n][:])
                    nc.sync.dma_start(out_rows[:, n, m0 : m0 + width], rows[:])
                else:
                    copy = nc.vector.tensor_copy if c == len(CHUNKS) - 1 and n % 2 else nc.scalar.copy
                    copy(result[:, n, :], banks[c][n][:])
            if c > 0:
                nc.sync.dma_start(out_rows[:, :, m0 : m0 + width], result[:])

        pieces = []
        for m0, width in STRETCHES:
            pieces.append((0, m0, width))
            pieces.extend((1,) + chunk for chunk in CHUNKS if m0 <= chunk[0] < m0 + width)

        def multiply(u, grouped):
            b, m0, width = pieces[u]
            x_q = quantize(grouped, "x_codes%d" % u, "x_sc%d" % u)
            for c, chunk in enumerate(CHUNKS):
                if m0 <= chunk[0] < m0 + width:
                    if b == 0:
                        open_chunk(c, x_q, m0)
                    else:
                        close_chunk(c, x_q)

        waiting = None
        for u, (b, m0, width) in enumerate(pieces):
            picked = pick(b, m0, width, ("late_room", "grouped1")[u % 2])
            grouped = held([P, PACK * width], BF16, ("repeats", "tab_sb")[u % 2])[:]
            if u == len(pieces) - 1:
                multiply(u - 1, waiting)
                interleave(nc.vector.tensor_copy, grouped, picked[:])
            else:
                interleave(nc.scalar.copy, grouped, picked[:])
                if u > 0:
                    multiply(u - 1, waiting)
            waiting = grouped
        multiply(len(pieces) - 1, waiting)
